import numpy as np, ml_dtypes
CORES = [2,7,18,23,34]
N = 5
BF = ml_dtypes.bfloat16
def gentries(a):
    return np.ascontiguousarray(a.reshape(8, 16, -1).transpose(0, 2, 1)).reshape(8, -1)
def gtable(e):
    e = np.asarray(e); return np.ascontiguousarray(e.reshape(8, -1, 16).transpose(0, 2, 1)).reshape(128, -1).astype(np.int32)
V, D, M, R = 2048, 3, 96, 3
def joined(x):
    return np.stack([gentries(x[r]).reshape(8, D, V) for r in range(N)], 2).reshape(8, D, N * V)
def pack(p, a, w):
    pin, inc = [np.stack([gtable(x.reshape(8, D, N, V)[:, :, r].reshape(8, D * V)) for r in range(N)]) for x in (p, np.argsort(p, -1))]
    return {"part": np.ascontiguousarray(a.transpose(1, 0, 2)).astype(np.int32), "pin": pin, "inc": inc, "w": np.ascontiguousarray(w).astype(np.int32)}
def mix(rng, p, share):
    p = np.array(p); s = np.flatnonzero(rng.random(p.size) < share); p[s] = rng.permutation(p[s]); return p
def clusters(rng, noise):
    p = np.zeros((8, D, N * V), np.int64); h = rng.integers(0, 16, (8, N * V))
    for g in range(8):
        e = np.argsort(rng.permutation(h[g]), kind="stable")
        for i in range(D):
            p[g, i, e] = np.lexsort((rng.random(N * V), h[g])); p[g, i] = mix(rng, p[g, i], noise[g])
    return p, h
def spoil(rng, h, share):
    return np.where(rng.random((8, N, V)) < share, rng.integers(0, 16, (8, N, V)), h.reshape(8, N, V))
def setup_inputs(rng):
    p, h = clusters(rng, rng.random(8) * 0.15)
    return pack(p, spoil(rng, h, rng.random((8, N, 1)) * 0.3), rng.integers(0, 16, (N, 8, V)))
def setup_inputs_ties(rng):
    p = np.stack([np.stack([rng.permutation(N * V) for i in range(D)]) for g in range(8)])
    w = rng.integers(1, 16, (1, 8, 1)) * np.where(np.arange(8)[None, :, None] & 1, rng.integers(0, 2, (N, 8, V)), 1)
    return pack(p, rng.integers(0, 16, (8, N, V)), w)
def setup_inputs_cap(rng):
    n = rng.random(8) * 0.15; n[:3] = 0; p, h = clusters(rng, n); a = spoil(rng, h, rng.random((8, N, 1)) * 0.3)
    w = rng.integers(0, 16, (N, 8, V)); w[:, :3] = np.maximum(w[:, :3], 1); inv = np.argsort(p, -1)
    for g in range(3):
        m = np.array(h[g]); busy = np.zeros(N * V, bool); want = np.roll(np.array([M, M + 1, M - 1, 0, M, 1, M + 1, M // 2])[:N], g)
        for r in range(N):
            left = int(want[r])
            for v in rng.permutation(V // 2) * 2 + (r * V + (g == 2)):
                if left == 0: break
                e = inv[g, :, v]
                if busy[e].any() or len(set(e.tolist())) < D: continue
                busy[e] = True; m[v] = (h[g, v] + rng.integers(1, 16)) & 15; left -= 1
        a[g] = m.reshape(N, V)
    return pack(p, a, w)
def setup_inputs_twins(rng):
    p = np.zeros((8, D, N * V), np.int64); j = np.arange(N * V); a = np.zeros((8, N, V), np.int64)
    for g in range(8):
        b = j if g == 0 else (j + V) % (N * V) if g == 1 else rng.permutation(N * V); s = 0.3 + 0.5 * rng.random()
        for i in range(D): p[g, i] = b if i == 0 else mix(rng, b, s)
        u = rng.permutation(16)[:rng.integers(2, 17)]; a[g] = u[rng.integers(0, u.size, (N, V))]
    return pack(p, a, rng.integers(0, 16, (N, 8, V)))
def setup_inputs_spread(rng):
    p, h = clusters(rng, rng.random(8)); k = 2.0 ** rng.integers(0, 5, (8, N, 1))
    q = np.minimum((16 * rng.random((8, N, V)) ** k).astype(np.int64), 15)
    a = np.where(rng.random((8, N, V)) < rng.random((8, N, 1)), q, h.reshape(8, N, V))
    w = np.where(rng.random((N, 8, V)) < rng.random((N, 8, 1)), rng.choice(np.array([0, 15]), (N, 8, V)), rng.integers(0, 16, (N, 8, V)))
    return pack(p, a, w)
def check_inputs(d):
    bad = [n for n, top in (("part", 16), ("pin", N * V), ("inc", N * V), ("w", 16)) if np.min(d[n]) < 0 or np.max(d[n]) >= top]
    if not bad:
        p, q, j = joined(d["pin"]), joined(d["inc"]), np.arange(N * V)
        if (np.sort(p, -1) != j).any(): bad.append("every vertex once at each position of pin")
        elif (np.take_along_axis(q, p, -1) != j).any(): bad.append("inc is the inverse of pin")
    return bad
def counts(a, p):
    return np.sum(a[p][None] == np.arange(16)[:, None, None], 1)
def reference(part, pin, inc, w):
    a = np.array(part.transpose(1, 0, 2)).reshape(8, N * V).astype(np.int64); wt = np.array(w.transpose(1, 0, 2)).reshape(8, N * V).astype(np.int64)
    p, e, j = joined(pin), joined(inc), np.arange(N * V); cut = np.zeros(8, np.int64)
    for g in range(8):
        for t in range(R):
            c = counts(a[g], p[g]); one = wt[g] * (c == 1); none = wt[g] * (c == 0)
            gain = np.sum(one[np.broadcast_to(a[g], (D, N * V)), e[g]], 0) - np.sum(none[:, e[g]], 1)
            gain[a[g], j] = -1000000
            best = np.argmax(gain, 0)
            can = ((gain[best, j] > 0) & (((j % V) + t) % 2 == 0)).reshape(N, V)
            go = (can & (np.add.accumulate(can.astype(np.int64), 1) <= M)).reshape(-1)
            a[g] = np.where(go, best, a[g])
        cut[g] = np.sum(wt[g] * (np.sum(counts(a[g], p[g]) > 0, 0) - 1))
    return {"newpart": np.ascontiguousarray(a.reshape(8, N, V).transpose(1, 0, 2)).astype(np.float32), "cut": np.repeat(cut.astype(np.float32)[None, :, None], N, 0)}

@@ -1,0 +1,532 @@
+from concourse.bass import DstId, RemoteDMATransfer
+from concourse.mybir import AluOpType as A, AxisListType, ActivationFunctionType as F
+
+N, V, M, R = 5, 2048, 96, 3
+NV = N * V
+XV = 640
+SCRATCH = {"land": ("sbuf", [128, N, 2, 640], "bfloat16")}
+for _t, _l in (("bfloat16", dict(tab=NV, win=NV, gat=3 * V, pb=256, wp=4096, tt=2048, uu=2048, ca=4096, zz=2048, zero=512, st=256,
+                                 xl=R * N * 128, cand=64, gd=128, ident=128, ip32=128, im32=128, im1=128, tri=128, ones=128,
+                                 own=128, selw=128, prm=64, i64=64, zj=432, sel=1024)),
+               ("int32", dict(m32=512, wl=2040, inc32=384, p32=256, i0=384, i1=384, ki=64, kr=64, row=4)),
+               ("uint16", dict(ioff=384, noff=768)),
+               ("float32", dict(ks=1024, rst=512, thr=64, dl=64, go=64, outp=256, cl=8 * N, cs=4, cd=144, cgr=128, c15=128, cpj=64,
+                                cj=4, co=16, col=16, e1=4, e2=4, posf=384, csp=128, spl=512, sq=64, bst=64, bm=128, gz=8))):
+    for _n in _l:
+        SCRATCH[_n] = ("sbuf", [128, _l[_n]], _t)
+for _n in ("K0", "K1", "Y0", "Y1", "U0", "U1", "SM", "PO"):
+    SCRATCH[_n] = ("psum", [128, 512], "float32")
+SEMAPHORES = (["cv", "cs", "cp", "cg", "ls", "ldp", "ldw", "ldi", "ldx", "wd", "so", "sc", "ac"] + ["pf%d" % q for q in range(N)]
+              + ["ax%d_%d" % (k, q) for k in range(R) for q in range(N)] + ["pd%d_%d" % (h, q) for h in range(2) for q in range(N)])
+
+
+def rank_program(g, core, T, topo):
+    me = T.rank_of(core)
+    if me is None:
+        return
+    cores = list(T.cores)
+    Q = {"v": g.vector, "s": g.scalar, "p": g.tensor, "g": g, "y": g.sync}
+    vec, act, pe = g.vector, g.scalar, g.tensor
+    total, seen, wr, rd = {}, {}, {}, {}
+
+    def wait(q, tok):
+        if seen.get((q, tok[0]), 0) < tok[1]:
+            Q[q].wait_ge(T.sem[tok[0]], tok[1])
+            seen[(q, tok[0])] = tok[1]
+
+    def deps(q, r, w, toks):
+        need = list(toks) + [wr[k] for k in list(r) + list(w) if k in wr]
+        for k in w:
+            need += rd.get(k, [])
+        best = {}
+        for s, n in need:
+            if not (q == "p" and s == "cp"):
+                best[s] = max(best.get(s, 0), n)
+        for s in best:
+            wait(q, (s, best[s]))
+
+    def done(tok, r, w):
+        for k in r:
+            rd.setdefault(k, []).append(tok)
+        for k in w:
+            wr[k] = tok
+            rd[k] = []
+
+    def op(q, fn, r=(), w=(), toks=()):
+        deps(q, r, w, toks)
+        s = "c" + q
+        fn().then_inc(T.sem[s], 1)
+        total[s] = total.get(s, 0) + 1
+        done((s, total[s]), r, w)
+
+    def dmas(q, s, pairs, r=(), w=(), toks=()):
+        deps(q, r, w, toks)
+        for o, i in pairs:
+            Q[q].dma_start(o, i).then_inc(T.sem[s], 16)
+            total[s] = total.get(s, 0) + 16
+        done((s, total[s]), r, w)
+
+    def mms(lst, r, w, toks=()):
+        def run():
+            last = None
+            for o, l, rr, a, b in lst:
+                last = pe.matmul(o, l, rr, a, b)
+            return last
+        op("p", run, r, w, toks)
+
+    def chip_ranks(q):
+        return [x for x in range(N) if topo.chip(cores[x]) == topo.chip(cores[q])]
+
+    def near_engines(src, dst):
+        far = [x for x in range(N) if x not in chip_ranks(src)]
+        keep = topo.engines(cores[src], cores[far[0]])
+        return [e for e in topo.engines(cores[src], cores[dst]) if e not in keep]
+
+    def masks(src, dsts):
+        far = [d for d in dsts if d not in chip_ranks(src)]
+        near = [d for d in dsts if d in chip_ranks(src)]
+        out = {}
+        for part in (far, near):
+            if not part:
+                continue
+            free = topo.engines(cores[src], cores[part[0]]) if part is far else near_engines(src, part[0])
+            for n, d in list(enumerate(part))[::-1]:
+                k = 1
+                while 2 * k * (n + 1) <= len(free):
+                    k *= 2
+                out[d], free = free[:k], free[k:]
+        return out
+
+    def send(items, r, toks=()):
+        deps("g", r, (), toks)
+        tr = []
+        for d, eng, s, src, dst in items:
+            assert topo.may_write(core, cores[d])
+            rid, pid, _ = topo.addr(cores[d])
+            tr.append(RemoteDMATransfer(dst_ids=[DstId(rid=rid, pnc=pid)], dma_engine_mask=sum(1 << e for e in eng),
+                                        remote_sem=T.sem[s], src=src, dst=dst))
+            total["ls"] = total.get("ls", 0) + len(eng)
+        g.remote_dma_fused(tr, local_sem=T.sem.ls)
+
+    others = [q for q in range(N) if q != me]
+    mine = chip_ranks(me)
+    order = [me] + [q for q in mine if q != me] + [q for q in others if q not in mine]
+
+    def half_dsts(src, h):
+        out = []
+        for q in range(N):
+            c = chip_ranks(q)
+            if q != src and (src in c or c[h % len(c)] == q):
+                out.append(q)
+        return out
+
+    def bcast(sem, ap):
+        mk = masks(me, others)
+        return [(d, mk[d], sem, ap, ap) for d in others]
+
+    def arr(sem, q):
+        n = len(masks(q, [x for x in range(N) if x != q])[me])
+        total[sem] = n
+        return (sem, n)
+
+    dmas("y", "ldx", [(T.p32[0:64, :], T.part[:])], w=["p32"])
+    dmas("y", "ldp", [(T.m32[32 * i:32 * i + 32, :], T.pin[:, 128 * i:128 * i + 128]) for i in range(3)], w=["m32"])
+    dmas("s", "ldw", [(T.wl[96 + u:128:4, 0:2036], T.w[:, 4 * u:4 * u + 2036]) for u in range(4)], w=["wl"])
+    dmas("y", "ldi", [(T.inc32[:], T.inc[:])], w=["inc32"])
+
+    def iota(out, pat, base, cm, key, fl=True):
+        if fl:
+            op("g", lambda: g.iota(out, pat, base, cm, allow_small_or_imprecise_dtypes=True), w=[key])
+        else:
+            op("g", lambda: g.iota(out, pat, base, cm), w=[key])
+    iota(T.cd[:], [[1, 144]], 0, -1, "cd")
+    iota(T.cpj[:], [[1, 8], [8, 8]], 0, -1, "cpj")
+    iota(T.row[:, 0:1], [[0, 1]], 0, 1, "row", False)
+    iota(T.co[0:64, :], [[32, 16]], 0, 0, "co0")
+    iota(T.cgr[:], [[16, 8], [0, 16]], 0, 0, "cgr")
+    iota(T.c15[:], [[0, 8], [-1, 16]], 15, 0, "c15")
+    iota(T.cj[:], [[1, 4]], 0, 0, "cj")
+    iota(T.csp[:], [[16, 8], [1000, 2], [2, 8]], 0, 0, "csp")
+
+    def ts(out, in0, s1, s2, o0, o1=None, r=(), w=()):
+        if o1 is None:
+            op("v", lambda: vec.tensor_scalar(out, in0, s1, None, o0), r, w)
+        else:
+            op("v", lambda: vec.tensor_scalar(out, in0, s1, s2, o0, o1), r, w)
+
+    def tt(out, in0, in1, o, r=(), w=()):
+        op("v", lambda: vec.tensor_tensor(out, in0, in1, o), r, w)
+
+    def cp(out, in_, r=(), w=()):
+        op("v", lambda: vec.tensor_copy(out, in_), r, w)
+
+    def ms(out, c, key):
+        op("v", lambda: vec.memset(out, c), w=[key])
+
+    def ac(out, in_, f, r=(), w=(), **kw):
+        op("s", lambda: act.activation(out, in_, f, **kw), r, w)
+
+    ms(T.win[:, 0:3072], 0.0, "wina")
+    ms(T.land[96:128, me, 1, 0:512], 0.0, "L0")
+    ts(T.ident[:], T.cd[:, 0:128], 0.0, None, A.is_equal, r=["cd"], w=["ident"])
+    ts(T.prm[:], T.cpj[:], 0.0, None, A.is_equal, r=["cpj"], w=["prm"])
+
+    cp(T.pb[0:64, :], T.p32[0:64, :], ["p32"], ["pb"])
+    mms([(T.SM[:, 64 * t:64 * t + 64], T.pb[0:64, t:256:2], T.prm[0:64, :], True, True) for t in range(2)], ["pb", "prm"], ["SM"])
+    for t in range(2):
+        ac(T.st[:, 128 * t:128 * t + 64], T.SM[:, 64 * t:64 * t + 64], F.Copy, ["SM"], ["x%d" % t])
+        ac(T.st[:, 128 * t + 64:128 * t + 128], T.SM[:, 64 * t:64 * t + 64], F.Square, ["SM"], ["xx%d" % t])
+    mms([(T.PO[:, 128 * t:128 * t + 128], T.st[:, 128 * t:128 * t + 128], T.ident[:], True, True) for t in range(2)],
+        ["x0", "x1", "xx0", "xx1", "ident"], ["PO"])
+    for t in range(2):
+        ac(T.land[:, me, t, 512:640], T.PO[:, 128 * t:128 * t + 128], F.Copy, ["PO"], ["m%d" % t])
+
+    cp(T.land[0:96, me, 0, 0:512], T.m32[0:96, :], ["m32"], ["H"])
+    for a in range(4):
+        cp(T.land[96:128, me, 0, 128 * a:128 * a + 128], T.wl[96:128, a:a + 2033:16], ["wl"], ["Hw%d" % a])
+    tt(T.land[0:96, me, 1, 0:512], T.m32[0:96, :], T.land[0:96, me, 0, 0:512], A.subtract, ["m32", "H"], ["L"])
+    hkeys = [["H"] + ["Hw%d" % a for a in range(4)], ["L", "L0"]]
+    for h in range(2):
+        ds = half_dsts(me, h)
+        mk = masks(me, ds)
+        ap = T.land[:, me, h, :]
+        send([(d, mk[d], "pd%d_%d" % (h, me), ap, ap) for d in ds], hkeys[h] + ["m%d" % h])
+    got = [{}, {}]
+    for h in range(2):
+        for q in others:
+            ds = half_dsts(q, h)
+            if me in ds:
+                s = "pd%d_%d" % (h, q)
+                total[s] = len(masks(q, ds)[me])
+                got[h][q] = (s, total[s])
+    iota(T.rst[:], [[0, 32], [1, 16]], 0, 0, "rst")
+
+    hs = [0, 1]
+    if len(mine) > 1:
+        h = mine.index(me)
+        hs = [h, 1 - h]
+        eng = near_engines(me, mine[1 - h])
+        for q in others:
+            if q not in mine:
+                send([(mine[1 - h], eng, "pf%d" % q, T.land[:, q, h, :], T.land[:, q, h, :])], [], [got[h][q]])
+                total["pf%d" % q] = len(eng)
+                got[1 - h][q] = ("pf%d" % q, len(eng))
+
+    c = T.col
+    ts(T.row[:, 1:2], T.row[:, 0:1], 15, None, A.bitwise_and, r=["row"], w=["row1"])
+    ms(T.co[64:128, :], -16.0, "co1")
+    tt(T.i64[:], T.ident[:, 0:64], T.ident[:, 64:128], A.add, ["ident"], ["i64"])
+    cp(c[:, 0:1], T.row[:, 1:2], ["row1"], ["p"])
+    for p in range(16):
+        ts(T.sel[:, p:1024:16], T.i64[:], T.co[:, p:p + 1], None, A.mult, r=["i64", "co0", "co1"], w=["sel%d" % p])
+    tt(c[:, 1:2], c[:, 0:1], c[:, 0:1], A.mult, ["p"], ["pp"])
+    ts(c[:, 2:3], c[:, 1:2], -16.0, 16.0, A.mult, A.add, ["pp"], ["bias"])
+    ms(T.win[:, 3072:NV], 0.0, "winb")
+    tt(c[:, 3:4], T.row[:, 0:1], T.row[:, 1:2], A.subtract, ["row", "row1"], ["g16"])
+    ts(c[:, 4:5], c[:, 0:1], -1.0, 15.0, A.mult, A.add, ["p"], ["p15"])
+    ts(T.e1[:], T.cj[:], c[:, 0:1], None, A.is_equal, r=["cj", "p"], w=["e1"])
+    ts(T.e2[:], T.cj[:], 4.0, c[:, 0:1], A.add, A.is_equal, ["cj", "p"], ["e2"])
+    ts(T.bm[:], T.cgr[:], c[:, 3:4], None, A.is_equal, r=["cgr", "g16"], w=["bm"])
+    for out, key, k in ((T.ip32, "ip32", 32.0), (T.im32, "im32", -32.0), (T.im1, "im1", -1.0)):
+        ts(out[:], T.cd[:, 0:128], 0.0, k, A.is_equal, A.mult, ["cd"], [key])
+    ts(T.tri[:], T.cd[:, 0:128], 0.0, None, A.is_ge, r=["cd"], w=["tri"])
+    ms(T.ones[:], 1.0, "ones")
+    ms(T.zero[:], 0.0, "zero")
+    ms(T.cl[:, 8 * me:8 * me + 8], 0.0, "cl")
+    tt(T.e2[:], T.e2[:], T.e1[:], A.add, ["e1"], ["e2"])
+    ts(c[:, 5:6], T.e1[:, 3:4], -15.0, None, A.mult, r=["e1"], w=["wsc"])
+    ts(T.selw[:], T.bm[:], T.e1[:, 3:4], None, A.mult, r=["bm", "e1"], w=["selw"])
+    ts(T.gz[:], T.bm[:, 0:128:16], -1.0, None, A.mult, r=["bm"], w=["gz"])
+    tt(T.c15[:], T.c15[:], T.bm[:], A.mult, ["bm"], ["c15"])
+    for j in range(3):
+        ts(T.zj[:, 144 * j:144 * j + 144], T.cd[:], c[:, 4:5], T.e2[:, j:j + 1], A.is_equal, A.mult, ["cd", "p15", "e2"], ["zj%d" % j])
+    ts(T.c15[:], T.c15[:], 0.0625, None, A.mult, w=["c15"])
+    ts(T.rst[:], T.rst[:], 0.0, -1000000.0, A.is_equal, A.mult, w=["rst"])
+    tt(T.own[:], T.c15[:], T.ident[:], A.add, ["c15", "ident"], ["own"])
+    cp(c[:, 6:7], T.row[:, 0:1], ["row"], ["rowf"])
+    for t in range(2):
+        for hi in range(2):
+            ts(T.spl[:, 256 * t + 128 * hi:256 * t + 128 * hi + 128], T.csp[:], float(t - 1000 * hi), c[:, 6:7], A.add, A.is_equal,
+               ["csp", "rowf"], ["spl%d" % (2 * t + hi)])
+
+    units = [(q, t) for q in order[:len(mine)] for t in range(2)] + [(q, t) for t in hs for q in order[len(mine):]]
+    for q, h in units:
+        deps("y", hkeys[h] + ["wina", "winb"], (), [] if q == me else [got[h][q]])
+        for i in range(4 - h):
+            g.sync.dma_start(T.win[4 * h + i:128:16, V * q:V * q + V], T.land[32 * i:32 * i + 32, q, h, 0:512]).then_inc(T.sem.wd, 16)
+            total["wd"] = total.get("wd", 0) + 16
+    done(("wd", total["wd"]), (), ["win"])
+
+    ts(T.i0[:], T.inc32[:], 15, None, A.bitwise_and, r=["inc32"], w=["i0"])
+    ts(T.i1[:], T.inc32[:], 4, 127, A.logical_shift_right, A.bitwise_and, ["inc32"], ["i1"])
+    ts(T.i0[:], T.i0[:], 127.0, None, A.mult, w=["i0"])
+    ts(T.i1[:], T.i1[:], -15.0, None, A.mult, w=["i1"])
+    tt(T.i0[:], T.i0[:], T.inc32[:], A.add, w=["i0"])
+    tt(T.posf[:], T.i0[:], T.i1[:], A.add, ["i0", "i1"], ["posf"])
+
+    selk = ["sel%d" % p for p in range(16)]
+    tabk = ["tab%d_%d_%d" % (q, t, hh) for q in range(N) for t in range(2) for hh in range(2)]
+    flip = {"v": 0, "s": 0}
+
+    def bank(e):
+        flip[e] ^= 1
+        return ("U%d" if e == "v" else "Y%d") % flip[e]
+
+    def update(e, q, t, hh, src, keys, toks):
+        b = bank(e)
+        mms([(T[b][:, 128 * s:128 * s + 128], T.sel[:, 128 * (4 * hh + s):128 * (4 * hh + s) + 128], src, True, True) for s in range(4)],
+            selk + keys, [b], toks)
+        out = T.tab[:, V * q + 1024 * hh + t:V * q + 1024 * hh + 1024:2]
+        key = "tab%d_%d_%d" % (q, t, hh)
+        if e == "v":
+            ts(out, T[b][:], c[:, 2:3], 0.0, A.add, A.max, ["bias"], [b, key])
+        else:
+            ac(out, T[b][:], F.Relu, ["bias"], [b, key], bias=c[:, 2:3])
+
+    n = 0
+    for q, t in units:
+        for hh in range(2):
+            if n == 12:
+                mms([(T.PO[:, 192 * z:192 * z + 192], T.spl[:, 256 * z + 128 * hi:256 * z + 128 * hi + 128], T.posf[:, hi:384:2],
+                      hi == 0, hi == 1) for z in range(2) for hi in range(2)], ["posf"] + ["spl%d" % z for z in range(4)], ["PO"])
+                cp(T.ioff[:], T.PO[:, 0:384], w=["PO", "ioff"])
+            update("v" if n >= 12 and n % 2 else "s", q, t, hh, T.land[:, q, t, 512:640], ["m%d" % t] if q == me else [],
+                   [] if q == me else [got[t][q]])
+            n += 1
+
+    def ncol(t, i, jj):
+        return 384 * t + 128 * i + 64 * jj
+
+    def gkeys(t, i):
+        return ["g%d_%d_0" % (t, i), "g%d_%d_1" % (t, i)]
+
+    def gcol(t, i):
+        return 3072 * t + 1024 * i
+
+    def setup_gather(t, i, e):
+        w, g0, o = T.win[:, 0:NV], gcol(t, i), 192 * t + 64 * i
+        for z in range(2):
+            out, src = T.gat[:, g0 + 512 * z:g0 + 512 * z + 512], w.indirect(T.ioff[:, o + 32 * z:o + 32 * z + 32])
+            if e[z] == "v":
+                cp(out, src, ["win", "ioff"], gkeys(t, i)[z:z + 1])
+            else:
+                ac(out, src, F.Copy, ["win", "ioff"], gkeys(t, i)[z:z + 1])
+
+    def lists_pe(t, i, b):
+        mms([(T[b][:, 64 * jj:64 * jj + 64], T.zj[:, 144 * j + 15 - a:144 * j + 143 - a], T.gat[:, gcol(t, i) + a:gcol(t, i) + 1024:16],
+              a == 0, a == 15) for jj, j in enumerate([x for x in range(3) if x != i]) for a in range(16)],
+            gkeys(t, i) + ["zj0", "zj1", "zj2"], [b])
+
+    def lists_ev(t, i, b):
+        cp(T.noff[:, ncol(t, i, 0):ncol(t, i, 0) + 128], T[b][:, 0:128], w=[b, "n%d_%d" % (t, i)])
+
+    def wrow(t, i, lo, n):
+        return T.gat[:, gcol(t, i) + lo:gcol(t, i) + lo + n]
+
+    def wprime(e, t, i, lo, n):
+        b = bank(e)
+        mms([(T[b][:, 0:n], T.selw[:], wrow(t, i, lo, n), True, True)], gkeys(t, i) + ["selw"], [b])
+        out = T.wp[:, 2048 * t + 1024 * i + lo:2048 * t + 1024 * i + lo + n]
+        key = "w%d_%d_%d" % (t, i, lo)
+        if e == "v":
+            ts(out, T[b][:, 0:n], -1.0, 16.0, A.mult, A.add, w=[b, key])
+        else:
+            ac(out, T[b][:, 0:n], F.Identity, w=[b, key], bias=16.0, scale=-1.0)
+
+    setup_gather(0, 0, "vs")
+    setup_gather(0, 2, "vs")
+    setup_gather(0, 1, "vs")
+    lists_pe(0, 0, "SM")
+    wprime("s", 0, 0, 0, 512)
+    lists_ev(0, 0, "SM")
+    lists_pe(0, 2, "PO")
+    wprime("s", 0, 0, 512, 512)
+
+    def slot(k, q):
+        return T.xl[:, (k * N + q) * 128:(k * N + q + 1) * 128]
+
+    def look(t, i, jj, lo, n):
+        return T.tab[:, 0:NV].indirect(T.noff[:, ncol(t, i, jj) + lo // 16:ncol(t, i, jj) + (lo + n) // 16])
+
+    def owncols(t, lo, n):
+        return T.tab[:, V * me + 2 * lo + t:V * me + 2 * (lo + n):2]
+
+    def sgather(e, t, i, jj, lo, n, c0):
+        if e == "v":
+            cp(T.ca[:, c0:c0 + n], look(t, i, jj, lo, n), tabk + ["n%d_%d" % (t, i)], ["ca%d" % c0])
+        else:
+            ac(T.ca[:, c0:c0 + n], look(t, i, jj, lo, n), F.Copy, tabk + ["n%d_%d" % (t, i)], ["ca%d" % c0])
+
+    for rnd in range(R):
+        t = rnd % 2
+        x, xx = T.st[:, 128 * t:128 * t + 64], T.st[:, 128 * t + 64:128 * t + 128]
+
+        def vt(i, lo, n):
+            tt(T.tt[:, 1024 * i + lo:1024 * i + lo + n], look(t, i, 0, lo, n), T.wp[:, 2048 * t + 1024 * i + lo:2048 * t + 1024 * i + lo + n],
+               A.max, tabk + ["n%d_%d" % (t, i), "w%d_%d_%d" % (t, i, lo)], ["t%d_%d" % (i, lo)])
+
+        def vu(i, lo, n):
+            tt(T.uu[:, 1024 * i + lo:1024 * i + lo + n], look(t, i, 1, lo, n), T.tt[:, 1024 * i + lo:1024 * i + lo + n],
+               A.max, tabk + ["n%d_%d" % (t, i), "t%d_%d" % (i, lo)], ["u%d_%d" % (i, lo)])
+
+        def kadd(src, c0, lo, n, mat, keys, stop=False):
+            b = "K%d" % (lo // 512)
+            mms([(T[b][:, lo % 512 + s:lo % 512 + s + 128], src[:, c0 + s:c0 + s + 128], mat[:], False, stop and s == n - 128)
+                 for s in range(0, n, 128)], keys, [b])
+
+        def kstart(h):
+            b = "K%d" % h
+            mms([(T[b][:], T.ident[:], T.zero[:], True, False)]
+                + [(T[b][:, 128 * s:128 * s + 128], owncols(t, 512 * h + 128 * s, 128), T.own[:], False, False) for s in range(4)],
+                ["ident", "zero", "own"] + tabk, [b])
+
+        def ya(b, i, lo, n, c0):
+            mms([(T[b][:, 0:n], T.selw[:], wrow(t, i, lo, n), True, False), (T[b][:, 0:n], T.im1[:], T.ca[:, c0:c0 + n], False, False)],
+                gkeys(t, i) + ["selw", "im1", "ca%d" % c0], [b])
+
+        def yb(b, n, c0):
+            mms([(T[b][:, 0:n], T.im1[:], T.ca[:, c0:c0 + n], False, True)], ["ca%d" % c0], [b])
+
+        def relu(b, n, z0):
+            ac(T.zz[:, z0:z0 + n], T[b][:, 0:n], F.Relu, w=[b, "z%d" % z0])
+
+        def scan(h):
+            b = "K%d" % h
+            op("v", lambda: vec.tensor_tensor_scan(T.ks[:, 512 * h:512 * h + 512], T.rst[:], T[b][:], 0.0, A.add, A.max), ["rst"], [b, "ks%d" % h])
+
+        xs, nx = 1024 - XV, XV - 512
+        if rnd > 0:
+            kstart(0)
+            kstart(1)
+            sgather("s", t, 2, 0, 0, 512, 0)
+            vt(0, 0, 512)
+        else:
+            vt(0, 0, 512)
+            lists_ev(0, 2, "PO")
+            sgather("s", t, 2, 0, 0, 512, 0)
+            wprime("v", 0, 1, 0, 512)
+            lists_pe(0, 1, "SM")
+            wprime("v", 0, 1, 512, nx)
+            kstart(0)
+            kstart(1)
+        ya("Y0", 2, 0, 512, 0)
+        sgather("s", t, 2, 1, 0, 512, 512)
+        vu(0, 0, 512)
+        if rnd == 0:
+            lists_ev(0, 1, "SM")
+        yb("Y0", 512, 512)
+        sgather("s", t, 2, 0, 512, 512, 1024)
+        vt(1, 0, 512)
+        kadd(T.uu, 0, 0, 512, T.ip32, ["u0_0", "ip32"])
+        ya("Y1", 2, 512, 512, 1024)
+        relu("Y0", 512, 0)
+        kadd(T.zz, 0, 0, 512, T.im32, ["z0", "im32"])
+        vu(1, 0, 512)
+        kadd(T.uu, 1024, 0, 512, T.ip32, ["u1_0"], True)
+        sgather("s", t, 2, 1, 512, 512, 1536)
+        vt(0, 512, 512)
+        yb("Y1", 512, 1536)
+        sgather("s", t, 1, 0, XV, xs, 2048)
+        vt(1, 512, nx)
+        ya("Y0", 1, XV, xs, 2048)
+        sgather("s", t, 1, 1, XV, xs, 2560)
+        yb("Y0", xs, 2560)
+        relu("Y1", 512, 512)
+        vu(0, 512, 512)
+        kadd(T.zz, 512, 512, 512, T.im32, ["z512"])
+        vu(1, 512, nx)
+        kadd(T.uu, 512, 512, 512, T.ip32, ["u0_512"])
+        kadd(T.uu, 1536, 512, nx, T.ip32, ["u1_512"])
+        scan(0)
+        relu("Y0", xs, 1024)
+        kadd(T.zz, 1024, XV, xs, T.im32, ["z1024"], True)
+        scan(1)
+        if rnd == 0:
+            for i in (0, 2, 1):
+                setup_gather(1, i, "ss")
+        ts(T.ki[:], T.ks[:, 15:1024:16], 2048.0, None, A.add, r=["ks0", "ks1"], w=["ki"])
+        ts(T.kr[:], T.ki[:], 31, None, A.bitwise_and, r=["ki"], w=["kr"])
+        ts(T.cand[:], T.kr[:], 16.0, None, A.is_lt, r=["kr"], w=["cand"])
+        mms([(T.SM[:, 0:64], T.tri[:], T.cand[:], True, False)]
+            + [(T.SM[:, 8 * d:64], T.ones[:], T.cand[:, 0:64 - 8 * d], False, d == 7) for d in range(1, 8)], ["cand", "tri", "ones"], ["SM"])
+        ts(T.bst[:], T.kr[:], -1.0, 15.0, A.mult, A.add, ["kr"], ["bst"])
+        ts(T.thr[:], T.cand[:], M + 1.5, -1.0, A.mult, A.add, ["cand"], ["thr"])
+        tt(T.sq[:], T.bst[:], T.bst[:], A.mult, ["bst"], ["sq"])
+        tt(T.dl[:], T.bst[:], x, A.subtract, ["bst", "x%d" % t], ["dl"])
+        tt(T.go[:], T.SM[:, 0:64], T.thr[:], A.is_le, ["thr"], ["SM", "go"])
+        tt(T.sq[:], T.sq[:], xx, A.subtract, ["xx%d" % t], ["sq"])
+        tt(T.gd[:, 0:64], T.go[:], T.dl[:], A.mult, ["go", "dl"], ["gd0"])
+        tt(T.gd[:, 64:128], T.go[:], T.sq[:], A.mult, ["go", "sq"], ["gd1"])
+        mms([(T.SM[:, 0:128], T.st[:, 128 * t:128 * t + 128], T.ident[:], True, False), (T.SM[:, 0:128], T.gd[:], T.ident[:], False, True)],
+            ["x%d" % t, "xx%d" % t, "gd0", "gd1"], ["SM"])
+        cp(slot(rnd, me), T.SM[:, 0:128], w=["SM", "msg"])
+        send(bcast("ax%d_%d" % (rnd, me), slot(rnd, me)), ["msg"])
+        if rnd > 0:
+            ac(T.outp[0:64, t:256:2], T.SM[0:64, 0:128], F.Copy, w=["SM", "out%d" % t])
+        if rnd == 0:
+            lists_pe(1, 0, "PO")
+            update("v", me, t, 0, slot(rnd, me), ["msg"], [])
+            update("v", me, t, 1, slot(rnd, me), ["msg"], [])
+            lists_ev(1, 0, "PO")
+            lists_pe(1, 2, "SM")
+            wprime("v", 1, 0, 0, 512)
+            wprime("v", 1, 0, 512, 512)
+            lists_ev(1, 2, "SM")
+            lists_pe(1, 1, "PO")
+            wprime("s", 1, 1, 0, 512)
+            wprime("s", 1, 1, 512, nx)
+            lists_ev(1, 1, "PO")
+            tt(T.st[:, 0:128], T.st[:, 0:128], T.gd[:], A.add, ["gd0", "gd1"], ["x0", "xx0"])
+        else:
+            update("v", me, t, 0, slot(rnd, me), ["msg"], [])
+            update("s", me, t, 1, slot(rnd, me), ["msg"], [])
+        if rnd == 1:
+            for z in range(2):
+                ac(T.zz[:, 0:1024], T.gat[:, gcol(z, 0):gcol(z, 0) + 1024], F.Identity, gkeys(z, 0) + ["wsc", "cl"],
+                   ["z0", "z512", "cl%d" % (4 + z)], scale=c[:, 5:6], accum_out=T.cl[:, 8 * me + 4 + z:8 * me + 5 + z])
+        if rnd == 2:
+            dmas("y", "so", [(T.newpart[:, 256 * s:256 * s + 256], T.outp[8 * s:8 * s + 8, :]) for s in range(8)], ["out0", "out1"])
+        for q in order[1:]:
+            for hh in range(2):
+                update("vs"[hh], q, t, hh, slot(rnd, q), [], [arr("ax%d_%d" % (rnd, q), q)])
+
+    cb = ["Y0", "Y1", "U0", "U1"]
+
+    def cya(u):
+        t, lo, b = u // 2, 512 * (u % 2), cb[u]
+        mms([(T[b][:], T.selw[:], wrow(t, 0, lo, 512), True, False), (T[b][:], T.im1[:], owncols(t, lo, 512), False, False)], tabk, [b])
+
+    def cr(u):
+        ac(T.zz[:, 512 * u:512 * u + 512], T[cb[u]][:], F.Relu, ["cl"], [cb[u], "z%d" % (512 * u), "cl%d" % u],
+           accum_out=T.cl[:, 8 * me + u:8 * me + u + 1])
+
+    def cg(e, u, jj, stop):
+        c0 = 1024 * u + 512 * jj
+        sgather(e, u // 2, 0, jj, 512 * (u % 2), 512, c0)
+        mms([(T[cb[u]][:], T.im1[:], T.ca[:, c0:c0 + 512], False, stop)], ["ca%d" % c0], [cb[u]])
+    cya(0)
+    cg("v", 0, 0, False)
+    cg("s", 0, 1, True)
+    cya(1)
+    cg("v", 1, 0, False)
+    cg("s", 1, 1, True)
+    cya(2)
+    cya(3)
+    cg("v", 2, 0, False)
+    cg("s", 2, 1, True)
+    cr(0)
+    cg("v", 3, 0, False)
+    cr(1)
+    cg("v", 3, 1, True)
+    cr(2)
+    cr(3)
+    clk = ["cl"] + ["cl%d" % u for u in range(6)]
+    send(bcast("ac", T.cl[:, 8 * me:8 * me + 8]), clk)
+    total["ac"] = sum(len(masks(q, [z for z in range(N) if z != q])[me]) for q in others)
+    mms([(T.SM[0:8, 0:8 * N], T.gz[:], T.cl[:], True, True)], ["gz"] + clk, ["SM"], [("ac", total["ac"])])
+    op("v", lambda: vec.tensor_reduce(T.cs[0:8, 0:1], T.SM[0:8, 0:8 * N], AxisListType.X, A.add), w=["SM", "cs"])
+    dmas("y", "sc", [(T.cut[:], T.cs[0:8, 0:1])], ["cs"])
+    for s in total:
+        if s != "sc":
+            wait("g", (s, total[s]))
+    wait("g", ("sc", total["sc"]))

@@ -3,20 +3,21 @@ from concourse.mybir import AluOpType as A, AxisListType, ActivationFunctionType
 
 N, V, M, R = 5, 2048, 96, 3
 NV = N * V
-XV = 640
-SCRATCH = {"land": ("sbuf", [128, N, 2, 640], "bfloat16")}
-for _t, _l in (("bfloat16", dict(tab=NV, win=NV, gat=3 * V, pb=256, wp=4096, tt=2048, uu=2048, ca=4096, zz=2048, zero=512, st=256,
-                                 xl=R * N * 128, cand=64, gd=128, ident=128, ip32=128, im32=128, im1=128, tri=128, ones=128,
-                                 own=128, selw=128, prm=64, i64=64, zj=432, sel=1024)),
-               ("int32", dict(m32=512, wl=2040, inc32=384, p32=256, i0=384, i1=384, ki=64, kr=64, row=4)),
+XV = 704
+CV = 128
+SCRATCH = {"land": ("sbuf", [128, N, 768], "bfloat16"), "sel": ("sbuf", [128, 128, 16], "bfloat16")}
+for _t, _l in (("bfloat16", dict(tab=NV, win=NV, gat=3 * V, pb=256, wp=4096, tt=2048, uu=2048, ca=4096, zz=2048, kc=512, wb=128, wt=128,
+                                 xl=R * N * 64, cand=192, rp=192, kq=64, go=64, gd=64, idw=160, kl=128, zb=144, spl=512, pq=1152,
+                                 i16=128, im64=128, im1=128, tri=128, ones=192, selw=128, prm=192, zj=864, sw=512, c32=64, gz=8, gw=8, bm=128)),
+               ("int32", dict(m32=384, wl=128, inc32=384, p32=256, i0=384, i1=384, row=4)),
                ("uint16", dict(ioff=384, noff=768)),
-               ("float32", dict(ks=1024, rst=512, thr=64, dl=64, go=64, outp=256, cl=8 * N, cs=4, cd=144, cgr=128, c15=128, cpj=64,
-                                cj=4, co=16, col=16, e1=4, e2=4, posf=384, csp=128, spl=512, sq=64, bst=64, bm=128, gz=8))):
+               ("float32", dict(ks=1024, rst=512, dd=256, outp=128, cl=4 * N, cs=4, col=24, cj=4))):
     for _n in _l:
         SCRATCH[_n] = ("sbuf", [128, _l[_n]], _t)
 for _n in ("K0", "K1", "Y0", "Y1", "U0", "U1", "SM", "PO"):
     SCRATCH[_n] = ("psum", [128, 512], "float32")
-SEMAPHORES = (["cv", "cs", "cp", "cg", "ls", "ldp", "ldw", "ldi", "ldx", "wd", "so", "sc", "ac"] + ["pf%d" % q for q in range(N)]
+SEMAPHORES = (["cv", "cs", "cp", "cg", "ls", "ldp", "ldw", "ldi", "ldx", "wd", "so", "sc", "wz", "wr0", "wr1", "ac", "pn"]
+              + ["pf%d" % q for q in range(N)]
               + ["ax%d_%d" % (k, q) for k in range(R) for q in range(N)] + ["pd%d_%d" % (h, q) for h in range(2) for q in range(N)])
 
 
@@ -74,79 +75,11 @@ def rank_program(g, core, T, topo):
             return last
         op("p", run, r, w, toks)
 
-    def chip_ranks(q):
-        return [x for x in range(N) if topo.chip(cores[x]) == topo.chip(cores[q])]
-
-    def near_engines(src, dst):
-        far = [x for x in range(N) if x not in chip_ranks(src)]
-        keep = topo.engines(cores[src], cores[far[0]])
-        return [e for e in topo.engines(cores[src], cores[dst]) if e not in keep]
-
-    def masks(src, dsts):
-        far = [d for d in dsts if d not in chip_ranks(src)]
-        near = [d for d in dsts if d in chip_ranks(src)]
-        out = {}
-        for part in (far, near):
-            if not part:
-                continue
-            free = topo.engines(cores[src], cores[part[0]]) if part is far else near_engines(src, part[0])
-            for n, d in list(enumerate(part))[::-1]:
-                k = 1
-                while 2 * k * (n + 1) <= len(free):
-                    k *= 2
-                out[d], free = free[:k], free[k:]
-        return out
-
-    def send(items, r, toks=()):
-        deps("g", r, (), toks)
-        tr = []
-        for d, eng, s, src, dst in items:
-            assert topo.may_write(core, cores[d])
-            rid, pid, _ = topo.addr(cores[d])
-            tr.append(RemoteDMATransfer(dst_ids=[DstId(rid=rid, pnc=pid)], dma_engine_mask=sum(1 << e for e in eng),
-                                        remote_sem=T.sem[s], src=src, dst=dst))
-            total["ls"] = total.get("ls", 0) + len(eng)
-        g.remote_dma_fused(tr, local_sem=T.sem.ls)
-
-    others = [q for q in range(N) if q != me]
-    mine = chip_ranks(me)
-    order = [me] + [q for q in mine if q != me] + [q for q in others if q not in mine]
-
-    def half_dsts(src, h):
-        out = []
-        for q in range(N):
-            c = chip_ranks(q)
-            if q != src and (src in c or c[h % len(c)] == q):
-                out.append(q)
-        return out
-
-    def bcast(sem, ap):
-        mk = masks(me, others)
-        return [(d, mk[d], sem, ap, ap) for d in others]
-
-    def arr(sem, q):
-        n = len(masks(q, [x for x in range(N) if x != q])[me])
-        total[sem] = n
-        return (sem, n)
-
-    dmas("y", "ldx", [(T.p32[0:64, :], T.part[:])], w=["p32"])
-    dmas("y", "ldp", [(T.m32[32 * i:32 * i + 32, :], T.pin[:, 128 * i:128 * i + 128]) for i in range(3)], w=["m32"])
-    dmas("s", "ldw", [(T.wl[96 + u:128:4, 0:2036], T.w[:, 4 * u:4 * u + 2036]) for u in range(4)], w=["wl"])
-    dmas("y", "ldi", [(T.inc32[:], T.inc[:])], w=["inc32"])
-
     def iota(out, pat, base, cm, key, fl=True):
         if fl:
             op("g", lambda: g.iota(out, pat, base, cm, allow_small_or_imprecise_dtypes=True), w=[key])
         else:
             op("g", lambda: g.iota(out, pat, base, cm), w=[key])
-    iota(T.cd[:], [[1, 144]], 0, -1, "cd")
-    iota(T.cpj[:], [[1, 8], [8, 8]], 0, -1, "cpj")
-    iota(T.row[:, 0:1], [[0, 1]], 0, 1, "row", False)
-    iota(T.co[0:64, :], [[32, 16]], 0, 0, "co0")
-    iota(T.cgr[:], [[16, 8], [0, 16]], 0, 0, "cgr")
-    iota(T.c15[:], [[0, 8], [-1, 16]], 15, 0, "c15")
-    iota(T.cj[:], [[1, 4]], 0, 0, "cj")
-    iota(T.csp[:], [[16, 8], [1000, 2], [2, 8]], 0, 0, "csp")
 
     def ts(out, in0, s1, s2, o0, o1=None, r=(), w=()):
         if o1 is None:
@@ -166,105 +99,176 @@ def rank_program(g, core, T, topo):
     def ac(out, in_, f, r=(), w=(), **kw):
         op("s", lambda: act.activation(out, in_, f, **kw), r, w)
 
-    ms(T.win[:, 0:3072], 0.0, "wina")
-    ms(T.land[96:128, me, 1, 0:512], 0.0, "L0")
-    ts(T.ident[:], T.cd[:, 0:128], 0.0, None, A.is_equal, r=["cd"], w=["ident"])
-    ts(T.prm[:], T.cpj[:], 0.0, None, A.is_equal, r=["cpj"], w=["prm"])
+    chips = sorted(set(topo.chip(x) for x in cores))
 
-    cp(T.pb[0:64, :], T.p32[0:64, :], ["p32"], ["pb"])
-    mms([(T.SM[:, 64 * t:64 * t + 64], T.pb[0:64, t:256:2], T.prm[0:64, :], True, True) for t in range(2)], ["pb", "prm"], ["SM"])
-    for t in range(2):
-        ac(T.st[:, 128 * t:128 * t + 64], T.SM[:, 64 * t:64 * t + 64], F.Copy, ["SM"], ["x%d" % t])
-        ac(T.st[:, 128 * t + 64:128 * t + 128], T.SM[:, 64 * t:64 * t + 64], F.Square, ["SM"], ["xx%d" % t])
-    mms([(T.PO[:, 128 * t:128 * t + 128], T.st[:, 128 * t:128 * t + 128], T.ident[:], True, True) for t in range(2)],
-        ["x0", "x1", "xx0", "xx1", "ident"], ["PO"])
-    for t in range(2):
-        ac(T.land[:, me, t, 512:640], T.PO[:, 128 * t:128 * t + 128], F.Copy, ["PO"], ["m%d" % t])
+    def chip_ranks(q):
+        return [x for x in range(N) if topo.chip(cores[x]) == topo.chip(cores[q])]
 
-    cp(T.land[0:96, me, 0, 0:512], T.m32[0:96, :], ["m32"], ["H"])
-    for a in range(4):
-        cp(T.land[96:128, me, 0, 128 * a:128 * a + 128], T.wl[96:128, a:a + 2033:16], ["wl"], ["Hw%d" % a])
-    tt(T.land[0:96, me, 1, 0:512], T.m32[0:96, :], T.land[0:96, me, 0, 0:512], A.subtract, ["m32", "H"], ["L"])
-    hkeys = [["H"] + ["Hw%d" % a for a in range(4)], ["L", "L0"]]
-    for h in range(2):
-        ds = half_dsts(me, h)
-        mk = masks(me, ds)
-        ap = T.land[:, me, h, :]
-        send([(d, mk[d], "pd%d_%d" % (h, me), ap, ap) for d in ds], hkeys[h] + ["m%d" % h])
-    got = [{}, {}]
-    for h in range(2):
-        for q in others:
-            ds = half_dsts(q, h)
-            if me in ds:
-                s = "pd%d_%d" % (h, q)
-                total[s] = len(masks(q, ds)[me])
-                got[h][q] = (s, total[s])
-    iota(T.rst[:], [[0, 32], [1, 16]], 0, 0, "rst")
+    def far_chips(q):
+        k = chips.index(topo.chip(cores[q]))
+        return [[x for x in range(N) if topo.chip(cores[x]) == ch] for ch in chips[k + 1:] + chips[:k]]
 
-    hs = [0, 1]
-    if len(mine) > 1:
-        h = mine.index(me)
-        hs = [h, 1 - h]
-        eng = near_engines(me, mine[1 - h])
-        for q in others:
-            if q not in mine:
-                send([(mine[1 - h], eng, "pf%d" % q, T.land[:, q, h, :], T.land[:, q, h, :])], [], [got[h][q]])
-                total["pf%d" % q] = len(eng)
-                got[1 - h][q] = ("pf%d" % q, len(eng))
+    def far_order(q):
+        k = chip_ranks(q).index(q)
+        fc = [c[k % len(c):] + c[:k % len(c)] for c in far_chips(q)]
+        return [c[n] for n in range(2) for c in fc if n < len(c)]
 
+    others = [q for q in range(N) if q != me]
+    mine = chip_ranks(me)
+    near = [q for q in mine if q != me]
+    far = far_order(me)
+    far_eng = topo.engines(core, cores[far[0]])
+    near_eng = [e for q in near for e in topo.engines(core, cores[q]) if e not in far_eng]
+    ne = len(far_eng)
+
+    def send(items, r, toks=()):
+        deps("g", r, (), toks)
+        tr = []
+        for ds, eng, s, ap in items:
+            ids = []
+            for d in ds:
+                assert topo.may_write(core, cores[d])
+                rid, pid, _ = topo.addr(cores[d])
+                ids.append(DstId(rid=rid, pnc=pid))
+            tr.append(RemoteDMATransfer(dst_ids=ids, dma_engine_mask=sum(1 << e for e in eng), remote_sem=T.sem[s], srcs=[ap], dsts=[ap] * len(ds)))
+            total["ls"] = total.get("ls", 0) + len(eng)
+        g.remote_dma_fused(tr, local_sem=T.sem.ls)
+
+    def bcast(sem, ap):
+        return [(far, far_eng, sem, ap)] + ([(near, near_eng, sem, ap)] if near else [])
+
+    def arr(sem):
+        total[sem] = ne
+        return (sem, ne)
+
+    dmas("y", "ldx", [(T.p32[0:64, :], T.part[:])], w=["p32"])
+    dmas("s", "ldp", [(T.m32[:], T.pin[:])], w=["m32"])
+    dmas("y", "ldw", [(T.wl[:, 64 * u:64 * u + 64], T.w[u:8:2, :]) for u in range(2)], w=["wl"])
+    dmas("y", "ldi", [(T.inc32[:], T.inc[:])], w=["inc32"])
     c = T.col
-    ts(T.row[:, 1:2], T.row[:, 0:1], 15, None, A.bitwise_and, r=["row"], w=["row1"])
-    ms(T.co[64:128, :], -16.0, "co1")
-    tt(T.i64[:], T.ident[:, 0:64], T.ident[:, 64:128], A.add, ["ident"], ["i64"])
-    cp(c[:, 0:1], T.row[:, 1:2], ["row1"], ["p"])
-    for p in range(16):
-        ts(T.sel[:, p:1024:16], T.i64[:], T.co[:, p:p + 1], None, A.mult, r=["i64", "co0", "co1"], w=["sel%d" % p])
-    tt(c[:, 1:2], c[:, 0:1], c[:, 0:1], A.mult, ["p"], ["pp"])
-    ts(c[:, 2:3], c[:, 1:2], -16.0, 16.0, A.mult, A.add, ["pp"], ["bias"])
-    ms(T.win[:, 3072:NV], 0.0, "winb")
-    tt(c[:, 3:4], T.row[:, 0:1], T.row[:, 1:2], A.subtract, ["row", "row1"], ["g16"])
-    ts(c[:, 4:5], c[:, 0:1], -1.0, 15.0, A.mult, A.add, ["p"], ["p15"])
-    ts(T.e1[:], T.cj[:], c[:, 0:1], None, A.is_equal, r=["cj", "p"], w=["e1"])
-    ts(T.e2[:], T.cj[:], 4.0, c[:, 0:1], A.add, A.is_equal, ["cj", "p"], ["e2"])
-    ts(T.bm[:], T.cgr[:], c[:, 3:4], None, A.is_equal, r=["cgr", "g16"], w=["bm"])
-    for out, key, k in ((T.ip32, "ip32", 32.0), (T.im32, "im32", -32.0), (T.im1, "im1", -1.0)):
-        ts(out[:], T.cd[:, 0:128], 0.0, k, A.is_equal, A.mult, ["cd"], [key])
-    ts(T.tri[:], T.cd[:, 0:128], 0.0, None, A.is_ge, r=["cd"], w=["tri"])
+    cP, cB, cM0, cM1, cK0, cK1, cD1, cL1, cL2, cD2, cW, cD3 = [c[:, k:k + 1] for k in range(12)]
+    cU2 = [c[:, 16:17], c[:, 17:18]]
+    ident = T.idw[:, 16:144]
+
+    def pick(out, in_, pat, cmp, fill, base, cm, r, w):
+        op("g", lambda: g.affine_select(out, in_, pat, cmp, fill, base, cm), r, w)
+
+    def wipe(q):
+        ms(T.win[:, V * q:V * q + V], 0.0, "win%d" % q)
+
     ms(T.ones[:], 1.0, "ones")
-    ms(T.zero[:], 0.0, "zero")
-    ms(T.cl[:, 8 * me:8 * me + 8], 0.0, "cl")
-    tt(T.e2[:], T.e2[:], T.e1[:], A.add, ["e1"], ["e2"])
-    ts(c[:, 5:6], T.e1[:, 3:4], -15.0, None, A.mult, r=["e1"], w=["wsc"])
-    ts(T.selw[:], T.bm[:], T.e1[:, 3:4], None, A.mult, r=["bm", "e1"], w=["selw"])
-    ts(T.gz[:], T.bm[:, 0:128:16], -1.0, None, A.mult, r=["bm"], w=["gz"])
-    tt(T.c15[:], T.c15[:], T.bm[:], A.mult, ["bm"], ["c15"])
-    for j in range(3):
-        ts(T.zj[:, 144 * j:144 * j + 144], T.cd[:], c[:, 4:5], T.e2[:, j:j + 1], A.is_equal, A.mult, ["cd", "p15", "e2"], ["zj%d" % j])
-    ts(T.c15[:], T.c15[:], 0.0625, None, A.mult, w=["c15"])
-    ts(T.rst[:], T.rst[:], 0.0, -1000000.0, A.is_equal, A.mult, w=["rst"])
-    tt(T.own[:], T.c15[:], T.ident[:], A.add, ["c15", "ident"], ["own"])
-    cp(c[:, 6:7], T.row[:, 0:1], ["row"], ["rowf"])
+    iota(T.row[:, 0:1], [[0, 1]], 0, 1, "row", False)
+    pick(T.idw[:], T.ones[:, 0:160], [[1, 160]], A.is_equal, 0.0, -16, -1, ["ones"], ["ident"])
+    pick(T.prm[:], T.ones[:], [[1000, 3], [1, 8], [8, 8]], A.is_equal, 0.0, -1000, -1, ["ones"], ["prm"])
+    iota(T.cj[:], [[2, 4]], 2, 0, "cj")
     for t in range(2):
         for hi in range(2):
-            ts(T.spl[:, 256 * t + 128 * hi:256 * t + 128 * hi + 128], T.csp[:], float(t - 1000 * hi), c[:, 6:7], A.add, A.is_equal,
-               ["csp", "rowf"], ["spl%d" % (2 * t + hi)])
+            pick(T.spl[:, 256 * t + 128 * hi:256 * t + 128 * hi + 128], T.ones[:, 0:128], [[16, 8], [1000, 2], [2, 8]], A.is_equal, 0.0,
+                 t - 1000 * hi, -1, ["ones"], ["spl%d" % (2 * t + hi)])
+    wipe(me)
+    ts(T.row[:, 1:2], T.row[:, 0:1], 16, None, A.bitwise_and, r=["row"], w=["row1"])
+    ts(T.row[:, 2:3], T.row[:, 0:1], 15, None, A.bitwise_and, r=["row"], w=["row2"])
+    ts(cM1, T.row[:, 1:2], 16.0, None, A.is_equal, r=["row1"], w=["m1"])
+    ts(cM0, T.row[:, 1:2], 0.0, None, A.is_equal, r=["row1"], w=["m0"])
+    cp(cP, T.row[:, 2:3], ["row2"], ["p"])
+    ms(T.zb[:], 0.0, "zb")
+    ms(T.cand[:, 0:128], 0.0, "cand0")
+    ms(T.rp[:, 0:128], 0.0, "rp0")
+    ms(T.cl[:, 4 * me:4 * me + 4], 0.0, "cl")
+    for gh in range(2):
+        for ah in range(2):
+            k, o = 2 * gh + ah, 16 - 16 * (gh - ah)
+            ac(T.sw[:, 128 * k:128 * k + 128], T.idw[:, o:o + 128], F.Identity, ["ident", "m0", "m1"], ["sw%d" % k], scale=[cM0, cM1][ah])
+    ac(cB, cP, F.Identity, ["p"], ["bias"], scale=-16.0)
 
-    units = [(q, t) for q in order[:len(mine)] for t in range(2)] + [(q, t) for t in hs for q in order[len(mine):]]
+    L = T.land
+    cp(T.pb[0:64, :], T.p32[0:64, :], ["p32"], ["pb"])
+    tt(T.dd[:, 0:128], T.m32[:, 128:256], T.m32[:, 0:128], A.subtract, ["m32"], ["d1"])
+    mms([m for t in range(2) for m in ((T.SM[:, 64 * t:64 * t + 64], T.prm[0:64, 0:128], T.pb[0:64, 128 + t:256:2], True, False),
+                                       (T.SM[:, 64 * t:64 * t + 64], T.prm[0:64, 64:192], T.pb[0:64, t:128:2], False, True))],
+        ["pb", "prm"], ["SM"])
+    ac(L[:, me, 0:128], T.SM[:, 0:128], F.Copy, w=["SM", "x"])
+    cp(L[:, me, 128:256], T.dd[:, 0:128], ["d1"], ["h1"])
+    cp(T.wb[:], T.wl[:], ["wl"], ["wb"])
+    tt(L[:, me, 256:384], T.dd[:, 0:128], L[:, me, 128:256], A.subtract, ["d1", "h1"], ["l1"])
+    op("v", lambda: vec.transpose(T.wt[:], T.wb[:]), ["wb"], ["wt"])
+    tt(T.dd[:, 128:256], T.m32[:, 256:384], T.m32[:, 0:128], A.subtract, ["m32"], ["d2"])
+    mms([(T.PO[:, 32 * (2 * rr + ah):32 * (2 * rr + ah) + 32], T.sw[:, 128 * (2 * gh + ah):128 * (2 * gh + ah) + 128],
+          T.wt[:, 64 * gh + 32 * rr:64 * gh + 32 * rr + 32], gh == 0, gh == 1) for rr in range(2) for ah in range(2) for gh in range(2)],
+        ["wt"] + ["sw%d" % k for k in range(4)], ["PO"])
+    cp(L[:, me, 384:512], T.dd[:, 128:256], ["d2"], ["h2"])
+    for k in range(4):
+        ac(L[:, me, 640 + k:768:4], T.PO[:, 32 * k:32 * k + 32], F.Copy, ["PO"], ["ww%d" % k])
+    tt(L[:, me, 512:640], T.dd[:, 128:256], L[:, me, 384:512], A.subtract, ["d2", "h2"], ["l2"])
+    hkeys = [["x", "h1", "l1"], ["h2", "l2"] + ["ww%d" % k for k in range(4)]]
+
+    def half(q, h):
+        return L[:, q, 384 * h:384 * h + 384]
+    for h in range(2):
+        send([([ch[h % len(ch)] for ch in far_chips(me)], far_eng, "pd%d_%d" % (h, me), half(me, h))], hkeys[h])
+    got = [{}, {}]
+    if near:
+        send([(near, near_eng, "pn", L[:, me, :])], [])
+        got[0][near[0]] = got[1][near[0]] = arr("pn")
+    pick(T.bm[:], T.ones[:, 0:128], [[-16, 8], [0, 16]], A.is_ge, 0.0, 0, 1, ["ones"], ["bm"])
+    pick(T.bm[:], T.bm[:], [[16, 8], [0, 16]], A.is_ge, 0.0, 15, -1, (), ["bm"])
+    iota(T.c32[:], [[32, 64]], 0, 0, "c32")
+    come = sorted(far, key=lambda q: [topo.chip(cores[ch[0]]) for ch in far_chips(q)].index(topo.chip(core)))
+    hs = [0, 1]
+    if near:
+        h = mine.index(me)
+        hs = [h, 1 - h]
+        for q in come:
+            got[h][q] = arr("pd%d_%d" % (h, q))
+            send([(near, near_eng, "pf%d" % q, half(q, h))], [], [got[h][q]])
+            got[1 - h][q] = arr("pf%d" % q)
+    else:
+        for q in come:
+            for h in range(2):
+                got[h][q] = arr("pd%d_%d" % (h, q))
+    iota(T.rst[:], [[0, 32], [20000, 16]], 0, 0, "rst")
+    iota(T.kc[:], [[0, 32], [-1, 16]], 16, 128, "kc")
+
+    copies = come[-3:]
+    dmas("y", "wz", [(T.win[:, V * q:V * q + V], T.win[:, V * me:V * me + V]) for q in copies], ["win%d" % me, "m32", "wl"], ["win%d" % q for q in copies])
+    cp(T.sel[:, :, 0:1], ident, ["ident"], ["sel"])
+    ts(c[:, 6:9], T.cj[:, 0:3], cP, None, A.is_gt, r=["cj", "p"], w=["D1"])
+    cp(T.sel[:, :, 1:2], T.sel[:, :, 0:1], w=["sel"])
+    cp(T.sel[:, :, 2:4], T.sel[:, :, 0:2], w=["sel"])
+    tt(c[:, 9:11], c[:, 7:9], c[:, 6:8], A.subtract, ["D1"], ["D2"])
+    cp(T.sel[:, :, 4:8], T.sel[:, :, 0:4], w=["sel"])
+    tt(cD3, cD2, cD1, A.subtract, ["D1", "D2"], ["D3"])
+    cp(T.sel[:, :, 8:16], T.sel[:, :, 0:8], w=["sel"])
+    for q in near + come:
+        if q not in copies:
+            wipe(q)
+    for out, key, k in ((T.i16, "i16", 16.0), (T.im64, "im64", -64.0), (T.im1, "im1", -1.0)):
+        ac(out[:], ident, F.Copy, ["ident"], [key], scale=k)
+    for t in range(2):
+        ac(cU2[t], cP, F.Identity, ["p"], ["u%d" % t], scale=2.0, bias=float(V * me + t))
+    ac(cK1, T.idw[:, 17:18], F.Identity, ["ident"], ["k1"], scale=96.0)
+    ac(cK0, T.idw[:, 16:17], F.Identity, ["ident", "k1"], ["k0"], scale=-95.0, bias=cK1)
+    ac(T.kl[:], T.ones[:, 0:128], F.Identity, ["ones", "k0"], ["kl"], scale=cK0)
+    pick(T.tri[:], T.ones[:, 0:128], [[1, 128]], A.is_ge, 0.0, 0, -1, ["ones"], ["tri"])
+    pick(T.tri[:], T.tri[:], [[1, 128]], A.not_equal, -199.0, 0, -1, (), ["tri"])
+
+    def by_group():
+        ac(T.zb[:, 15:143:16], T.bm[:, 0:128:16], F.Copy, ["bm"], ["zb"])
+        ac(T.selw[:], T.bm[:], F.Identity, ["bm", "D2"], ["selw"], scale=cW)
+        for k, col in enumerate((cD1, cD2, cD3)):
+            ac(T.zj[:, 144 * k:144 * k + 144], T.zb[:], F.Identity, ["zb", "D1", "D2", "D3"], ["zj%d" % k], scale=col)
+        ac(T.gz[:], T.bm[:, 0:128:16], F.Copy, ["bm"], ["gz"], scale=-1.0)
+        ac(T.gw[:], T.selw[:, 0:128:16], F.Copy, ["selw"], ["gw"], scale=15.0)
+        ts(T.zj[:, 432:864], T.zj[:, 0:432], -1.0, None, A.mult, r=["zj0", "zj1", "zj2"], w=["zjm"])
+
+    units = [(q, h) for q in [me] + near for h in range(2)] + [(q, h) for h in hs for q in come]
     for q, h in units:
-        deps("y", hkeys[h] + ["wina", "winb"], (), [] if q == me else [got[h][q]])
-        for i in range(4 - h):
-            g.sync.dma_start(T.win[4 * h + i:128:16, V * q:V * q + V], T.land[32 * i:32 * i + 32, q, h, 0:512]).then_inc(T.sem.wd, 16)
+        deps("y", hkeys[h], ["win%d" % q], [] if q == me else [got[h][q]])
+        for f in ((0, 1), (2, 3, 4))[h]:
+            g.sync.dma_start(T.win[f:128:16, V * q:V * q + V], L[:, q, 128 * f + 128:128 * f + 256]).then_inc(T.sem.wd, 16)
             total["wd"] = total.get("wd", 0) + 16
     done(("wd", total["wd"]), (), ["win"])
 
-    ts(T.i0[:], T.inc32[:], 15, None, A.bitwise_and, r=["inc32"], w=["i0"])
-    ts(T.i1[:], T.inc32[:], 4, 127, A.logical_shift_right, A.bitwise_and, ["inc32"], ["i1"])
-    ts(T.i0[:], T.i0[:], 127.0, None, A.mult, w=["i0"])
-    ts(T.i1[:], T.i1[:], -15.0, None, A.mult, w=["i1"])
-    tt(T.i0[:], T.i0[:], T.inc32[:], A.add, w=["i0"])
-    tt(T.posf[:], T.i0[:], T.i1[:], A.add, ["i0", "i1"], ["posf"])
-
-    selk = ["sel%d" % p for p in range(16)]
     tabk = ["tab%d_%d_%d" % (q, t, hh) for q in range(N) for t in range(2) for hh in range(2)]
     flip = {"v": 0, "s": 0}
 
@@ -274,25 +278,38 @@ def rank_program(g, core, T, topo):
 
     def update(e, q, t, hh, src, keys, toks):
         b = bank(e)
-        mms([(T[b][:, 128 * s:128 * s + 128], T.sel[:, 128 * (4 * hh + s):128 * (4 * hh + s) + 128], src, True, True) for s in range(4)],
-            selk + keys, [b], toks)
+        mms([(T[b][:, 128 * s + 64 * nh:128 * s + 64 * nh + 64], T.sel[:, 8 * (8 * nh + 4 * hh + s):8 * (8 * nh + 4 * hh + s) + 8, :],
+              src, True, True) for s in range(4) for nh in range(2)], ["sel"] + keys, [b], toks)
         out = T.tab[:, V * q + 1024 * hh + t:V * q + 1024 * hh + 1024:2]
         key = "tab%d_%d_%d" % (q, t, hh)
         if e == "v":
-            ts(out, T[b][:], c[:, 2:3], 0.0, A.add, A.max, ["bias"], [b, key])
+            ts(out, T[b][:], cP, 16.0, A.not_equal, A.mult, ["p"], [b, key])
         else:
-            ac(out, T[b][:], F.Relu, ["bias"], [b, key], bias=c[:, 2:3])
+            ac(out, T[b][:], F.Abs, ["bias"], [b, key], bias=cB, scale=16.0)
 
-    n = 0
-    for q, t in units:
-        for hh in range(2):
-            if n == 12:
-                mms([(T.PO[:, 192 * z:192 * z + 192], T.spl[:, 256 * z + 128 * hi:256 * z + 128 * hi + 128], T.posf[:, hi:384:2],
-                      hi == 0, hi == 1) for z in range(2) for hi in range(2)], ["posf"] + ["spl%d" % z for z in range(4)], ["PO"])
-                cp(T.ioff[:], T.PO[:, 0:384], w=["PO", "ioff"])
-            update("v" if n >= 12 and n % 2 else "s", q, t, hh, T.land[:, q, t, 512:640], ["m%d" % t] if q == me else [],
-                   [] if q == me else [got[t][q]])
-            n += 1
+    def first(e, q, t, hh):
+        update(e, q, t, hh, L[:, q, 64 * t:64 * t + 64], ["x"] if q == me else [], [] if q == me else [got[0][q]])
+
+    rest = [(q, k // 2, k % 2) for q in near + come for k in range(4)]
+    ts(T.i0[:], T.inc32[:], 15, None, A.bitwise_and, r=["inc32"], w=["i0"])
+    ts(T.i1[:], T.inc32[:], 2032, None, A.bitwise_and, r=["inc32"], w=["i1"])
+    ts(T.pq[:, 0:384], T.inc32[:], 393216.0 - 1023.5, None, A.add, r=["inc32"], w=["pq0"])
+    ts(T.pq[:, 384:768], T.i0[:], 128.0, None, A.mult, r=["i0"], w=["pq1"])
+    ts(T.pq[:, 768:1152], T.i1[:], 0.0625, None, A.mult, r=["i1"], w=["pq2"])
+    first("v", me, 0, 0)
+    first("v", me, 0, 1)
+    for u in rest[:2]:
+        first("s", *u)
+    mms([(T.PO[:, 192 * z:192 * z + 192], T.spl[:, 256 * z + 128 * hi:256 * z + 128 * hi + 128], T.pq[:, 384 * k + hi:384 * k + 384:2],
+          hi + k == 0, hi + k == 3) for z in range(2) for k in range(3) for hi in range(2)],
+        ["pq0", "pq1", "pq2"] + ["spl%d" % z for z in range(4)], ["PO"])
+    by_group()
+    for k in range(2):
+        first("s", *rest[2 + k])
+        first("v", me, 1, k)
+    ts(T.ioff[:], T.PO[:, 0:384], -393216.0, None, A.add, w=["PO", "ioff"])
+    for n, u in enumerate(rest[4:]):
+        first("sv"[n % 2], *u)
 
     def ncol(t, i, jj):
         return 384 * t + 128 * i + 64 * jj
@@ -312,38 +329,45 @@ def rank_program(g, core, T, topo):
             else:
                 ac(out, src, F.Copy, ["win", "ioff"], gkeys(t, i)[z:z + 1])
 
-    def lists_pe(t, i, b):
-        mms([(T[b][:, 64 * jj:64 * jj + 64], T.zj[:, 144 * j + 15 - a:144 * j + 143 - a], T.gat[:, gcol(t, i) + a:gcol(t, i) + 1024:16],
-              a == 0, a == 15) for jj, j in enumerate([x for x in range(3) if x != i]) for a in range(16)],
-            gkeys(t, i) + ["zj0", "zj1", "zj2"], [b])
+    DIFF = ((0, 1), (3, 2), (4, 5))
 
-    def lists_ev(t, i, b):
-        cp(T.noff[:, ncol(t, i, 0):ncol(t, i, 0) + 128], T[b][:, 0:128], w=[b, "n%d_%d" % (t, i)])
+    def lists_pe(t, i, b, js=(0, 1)):
+        lst = []
+        for jj in js:
+            out, j = T[b][:, 64 * jj:64 * jj + 64], DIFF[i][jj]
+            lst.append((out, ident, T.c32[:], True, False))
+            lst += [(out, T.zj[:, 144 * j + 15 - a:144 * j + 143 - a], T.gat[:, gcol(t, i) + a:gcol(t, i) + 1024:16], False, a == 15) for a in range(16)]
+        mms(lst, gkeys(t, i) + ["zj0", "zj1", "zj2", "zjm", "c32", "ident"], [b])
+
+    def lists_ev(t, i, b, js=(0, 1)):
+        ts(T.noff[:, ncol(t, i, js[0]):ncol(t, i, js[-1]) + 64], T[b][:, 64 * js[0]:64 * js[-1] + 64], cU2[t], None, A.add,
+           r=["u%d" % t], w=[b] + ["n%d_%d_%d" % (t, i, jj) for jj in js])
 
     def wrow(t, i, lo, n):
         return T.gat[:, gcol(t, i) + lo:gcol(t, i) + lo + n]
 
+    def wcol(t, i, lo, n):
+        return T.wp[:, 2048 * t + 1024 * i + lo:2048 * t + 1024 * i + lo + n]
+
+    def wkeys(t, i):
+        return ["w%d_%d_0" % (t, i), "w%d_%d_512" % (t, i)]
+
     def wprime(e, t, i, lo, n):
         b = bank(e)
         mms([(T[b][:, 0:n], T.selw[:], wrow(t, i, lo, n), True, True)], gkeys(t, i) + ["selw"], [b])
-        out = T.wp[:, 2048 * t + 1024 * i + lo:2048 * t + 1024 * i + lo + n]
         key = "w%d_%d_%d" % (t, i, lo)
         if e == "v":
-            ts(out, T[b][:, 0:n], -1.0, 16.0, A.mult, A.add, w=[b, key])
+            cp(wcol(t, i, lo, n), T[b][:, 0:n], w=[b, key])
         else:
-            ac(out, T[b][:, 0:n], F.Identity, w=[b, key], bias=16.0, scale=-1.0)
+            ac(wcol(t, i, lo, n), T[b][:, 0:n], F.Copy, w=[b, key])
 
-    setup_gather(0, 0, "vs")
-    setup_gather(0, 2, "vs")
-    setup_gather(0, 1, "vs")
-    lists_pe(0, 0, "SM")
-    wprime("s", 0, 0, 0, 512)
-    lists_ev(0, 0, "SM")
-    lists_pe(0, 2, "PO")
-    wprime("s", 0, 0, 512, 512)
+    def wspread(t, i0):
+        n = 1024 * (1 - i0) + XV
+        dmas("y", "wr%d" % t, [(T.wp[p:128:16, 2048 * t + 1024 * i0:2048 * t + 1024 * i0 + n], T.gat[4:128:16, gcol(t, i0):gcol(t, i0) + n]) for p in range(16)],
+             [k for i in range(i0, 2) for k in gkeys(t, i)], [k for i in range(i0, 2) for k in wkeys(t, i)])
 
     def slot(k, q):
-        return T.xl[:, (k * N + q) * 128:(k * N + q + 1) * 128]
+        return T.xl[:, (k * N + q) * 64:(k * N + q + 1) * 64]
 
     def look(t, i, jj, lo, n):
         return T.tab[:, 0:NV].indirect(T.noff[:, ncol(t, i, jj) + lo // 16:ncol(t, i, jj) + (lo + n) // 16])
@@ -351,180 +375,210 @@ def rank_program(g, core, T, topo):
     def owncols(t, lo, n):
         return T.tab[:, V * me + 2 * lo + t:V * me + 2 * (lo + n):2]
 
-    def sgather(e, t, i, jj, lo, n, c0):
-        if e == "v":
-            cp(T.ca[:, c0:c0 + n], look(t, i, jj, lo, n), tabk + ["n%d_%d" % (t, i)], ["ca%d" % c0])
-        else:
-            ac(T.ca[:, c0:c0 + n], look(t, i, jj, lo, n), F.Copy, tabk + ["n%d_%d" % (t, i)], ["ca%d" % c0])
+    def ownk(t):
+        return [k for k in tabk if k.startswith("tab%d_%d" % (me, t))]
 
+    def sgather(t, i, jj, lo, n, c0):
+        ac(T.ca[:, c0:c0 + n], look(t, i, jj, lo, n), F.Sign, tabk + ["n%d_%d_%d" % (t, i, jj)], ["ca%d" % c0])
+
+    def yb(b, n, c0, stop):
+        mms([(T[b][:, 0:n], T.i16[:], T.ca[:, c0:c0 + n], False, stop)], ["ca%d" % c0, "i16"], [b])
+
+    def kstart(t):
+        for h in range(2):
+            b = "K%d" % h
+            mms([(T[b][:], T.kl[:], T.kc[:], True, False)]
+                + [(T[b][:, 128 * s:128 * s + 128], owncols(t, 512 * h + 128 * s, 128), T.im1[:], False, False) for s in range(4)],
+                ["kl", "kc", "im1"] + ownk(t), [b])
+
+    kstart(0)
+    setup_gather(0, 0, "vs")
+    setup_gather(0, 2, "vs")
+    lists_pe(0, 0, "SM", [0])
+    setup_gather(0, 1, "vs")
+    wspread(0, 1)
+    lists_ev(0, 0, "SM", [0])
+    wprime("s", 0, 0, 0, 512)
+    lists_pe(0, 2, "PO", [0])
+    lists_ev(0, 2, "PO", [0])
+    wprime("v", 0, 0, 512, 512)
+    lists_pe(0, 2, "SM", [1])
+    lists_pe(0, 0, "PO", [1])
+
+    lands = near + sorted(far, key=lambda q: far_order(q).index(me))
+    xs = 1024 - XV
     for rnd in range(R):
         t = rnd % 2
-        x, xx = T.st[:, 128 * t:128 * t + 64], T.st[:, 128 * t + 64:128 * t + 128]
+        xold, xkey = (L[:, me, 64 * t:64 * t + 64], "x") if rnd < 2 else (slot(0, me), "msg0")
 
         def vt(i, lo, n):
-            tt(T.tt[:, 1024 * i + lo:1024 * i + lo + n], look(t, i, 0, lo, n), T.wp[:, 2048 * t + 1024 * i + lo:2048 * t + 1024 * i + lo + n],
-               A.max, tabk + ["n%d_%d" % (t, i), "w%d_%d_%d" % (t, i, lo)], ["t%d_%d" % (i, lo)])
+            tt(T.tt[:, 1024 * i + lo:1024 * i + lo + n], look(t, i, 0, lo, n), wcol(t, i, lo, n),
+               A.min, tabk + ["n%d_%d_0" % (t, i)] + wkeys(t, i), ["t%d_%d" % (i, lo)])
 
-        def vu(i, lo, n):
+        def vu(i, lo, n, tk):
             tt(T.uu[:, 1024 * i + lo:1024 * i + lo + n], look(t, i, 1, lo, n), T.tt[:, 1024 * i + lo:1024 * i + lo + n],
-               A.max, tabk + ["n%d_%d" % (t, i), "t%d_%d" % (i, lo)], ["u%d_%d" % (i, lo)])
+               A.min, tabk + ["n%d_%d_1" % (t, i), tk], ["u%d_%d" % (i, lo)])
 
-        def kadd(src, c0, lo, n, mat, keys, stop=False):
+        def kadd(src, c0, lo, keys, stop=False):
             b = "K%d" % (lo // 512)
-            mms([(T[b][:, lo % 512 + s:lo % 512 + s + 128], src[:, c0 + s:c0 + s + 128], mat[:], False, stop and s == n - 128)
-                 for s in range(0, n, 128)], keys, [b])
+            mms([(T[b][:, s:s + 128], src[:, c0 + s:c0 + s + 128], T.im64[:], False, stop and s == 384) for s in range(0, 512, 128)], keys + ["im64"], [b])
 
-        def kstart(h):
-            b = "K%d" % h
-            mms([(T[b][:], T.ident[:], T.zero[:], True, False)]
-                + [(T[b][:, 128 * s:128 * s + 128], owncols(t, 512 * h + 128 * s, 128), T.own[:], False, False) for s in range(4)],
-                ["ident", "zero", "own"] + tabk, [b])
+        def yw(b, i, lo, n):
+            mms([(T[b][:, 0:n], T.selw[:], wrow(t, i, lo, n), True, False)], gkeys(t, i) + ["selw"], [b])
 
-        def ya(b, i, lo, n, c0):
-            mms([(T[b][:, 0:n], T.selw[:], wrow(t, i, lo, n), True, False), (T[b][:, 0:n], T.im1[:], T.ca[:, c0:c0 + n], False, False)],
-                gkeys(t, i) + ["selw", "im1", "ca%d" % c0], [b])
-
-        def yb(b, n, c0):
-            mms([(T[b][:, 0:n], T.im1[:], T.ca[:, c0:c0 + n], False, True)], ["ca%d" % c0], [b])
-
-        def relu(b, n, z0):
-            ac(T.zz[:, z0:z0 + n], T[b][:, 0:n], F.Relu, w=[b, "z%d" % z0])
+        def relu(b, out, n, key):
+            ac(out, T[b][:, 0:n], F.Relu, w=[b, key], bias=-32.0)
 
         def scan(h):
             b = "K%d" % h
-            op("v", lambda: vec.tensor_tensor_scan(T.ks[:, 512 * h:512 * h + 512], T.rst[:], T[b][:], 0.0, A.add, A.max), ["rst"], [b, "ks%d" % h])
+            op("v", lambda: vec.tensor_tensor_scan(T.ks[:, 512 * h:512 * h + 512], T.rst[:], T[b][:], 0.0, A.min, A.max), ["rst"], [b, "ks%d" % h])
 
-        xs, nx = 1024 - XV, XV - 512
-        if rnd > 0:
-            kstart(0)
-            kstart(1)
-            sgather("s", t, 2, 0, 0, 512, 0)
-            vt(0, 0, 512)
-        else:
-            vt(0, 0, 512)
-            lists_ev(0, 2, "PO")
-            sgather("s", t, 2, 0, 0, 512, 0)
-            wprime("v", 0, 1, 0, 512)
-            lists_pe(0, 1, "SM")
-            wprime("v", 0, 1, 512, nx)
-            kstart(0)
-            kstart(1)
-        ya("Y0", 2, 0, 512, 0)
-        sgather("s", t, 2, 1, 0, 512, 512)
-        vu(0, 0, 512)
         if rnd == 0:
-            lists_ev(0, 1, "SM")
-        yb("Y0", 512, 512)
-        sgather("s", t, 2, 0, 512, 512, 1024)
-        vt(1, 0, 512)
-        kadd(T.uu, 0, 0, 512, T.ip32, ["u0_0", "ip32"])
-        ya("Y1", 2, 512, 512, 1024)
-        relu("Y0", 512, 0)
-        kadd(T.zz, 0, 0, 512, T.im32, ["z0", "im32"])
-        vu(1, 0, 512)
-        kadd(T.uu, 1024, 0, 512, T.ip32, ["u1_0"], True)
-        sgather("s", t, 2, 1, 512, 512, 1536)
-        vt(0, 512, 512)
-        yb("Y1", 512, 1536)
-        sgather("s", t, 1, 0, XV, xs, 2048)
-        vt(1, 512, nx)
-        ya("Y0", 1, XV, xs, 2048)
-        sgather("s", t, 1, 1, XV, xs, 2560)
-        yb("Y0", xs, 2560)
-        relu("Y1", 512, 512)
-        vu(0, 512, 512)
-        kadd(T.zz, 512, 512, 512, T.im32, ["z512"])
-        vu(1, 512, nx)
-        kadd(T.uu, 512, 512, 512, T.ip32, ["u0_512"])
-        kadd(T.uu, 1536, 512, nx, T.ip32, ["u1_512"])
+            lists_ev(0, 2, "SM", [1])
+            vt(0, 0, 512)
+            lists_ev(0, 0, "PO", [1])
+            vt(0, 512, 512)
+        else:
+            vt(0, 0, 1024)
+        sgather(t, 2, 0, 0, 512, 0)
+        if rnd < 2:
+            lists_pe(t, 1, "SM")
+        else:
+            kstart(0)
+        yw("Y0", 2, 0, 512)
+        yw("Y1", 2, 512, 512)
+        yb("Y0", 512, 0, False)
+        sgather(t, 2, 1, 0, 512, 512)
+        yb("Y0", 512, 512, True)
+        if rnd == 1:
+            kstart(1)
+        if rnd < 2:
+            lists_ev(t, 1, "SM")
+        if rnd == 0:
+            vu(0, 0, 512, "t0_0")
+            vu(0, 512, 512, "t0_512")
+        vt(1, 0, XV)
+        yw("SM", 1, XV, xs)
+        sgather(t, 2, 0, 512, 512, 1024)
+        yb("Y1", 512, 1024, False)
+        relu("Y0", T.zz[:, 0:512], 512, "z0")
+        if rnd > 0:
+            vu(0, 0, 512, "t0_0")
+        kadd(T.zz, 0, 0, ["z0"])
+        sgather(t, 2, 1, 512, 512, 1536)
+        kadd(T.uu, 0, 0, ["u0_0"])
+        yb("Y1", 512, 1536, True)
+        if rnd > 0:
+            vu(0, 512, 512, "t0_0")
+        sgather(t, 1, 0, XV, xs, 2048)
+        yb("SM", xs, 2048, False)
+        sgather(t, 1, 1, XV, xs, 2560)
+        kadd(T.uu, 512, 512, ["u0_512"])
+        yb("SM", xs, 2560, True)
+        vu(1, 0, 512, "t1_0")
+        relu("Y1", T.zz[:, 512:1024], 512, "z512")
+        kadd(T.uu, 1024, 0, ["u1_0"], True)
+        vu(1, 512, XV - 512, "t1_0")
+        kadd(T.zz, 512, 512, ["z512"])
+        relu("SM", T.uu[:, 1024 + XV:2048], xs, "u1_x")
         scan(0)
-        relu("Y0", xs, 1024)
-        kadd(T.zz, 1024, XV, xs, T.im32, ["z1024"], True)
+        kadd(T.uu, 1536, 512, ["u1_512", "u1_x"], True)
+        mms([(T.PO[:, 0:64], T.im1[:], xold, True, False)], [xkey, "im1"], ["PO"])
         scan(1)
         if rnd == 0:
-            for i in (0, 2, 1):
-                setup_gather(1, i, "ss")
-        ts(T.ki[:], T.ks[:, 15:1024:16], 2048.0, None, A.add, r=["ks0", "ks1"], w=["ki"])
-        ts(T.kr[:], T.ki[:], 31, None, A.bitwise_and, r=["ki"], w=["kr"])
-        ts(T.cand[:], T.kr[:], 16.0, None, A.is_lt, r=["kr"], w=["cand"])
-        mms([(T.SM[:, 0:64], T.tri[:], T.cand[:], True, False)]
-            + [(T.SM[:, 8 * d:64], T.ones[:], T.cand[:, 0:64 - 8 * d], False, d == 7) for d in range(1, 8)], ["cand", "tri", "ones"], ["SM"])
-        ts(T.bst[:], T.kr[:], -1.0, 15.0, A.mult, A.add, ["kr"], ["bst"])
-        ts(T.thr[:], T.cand[:], M + 1.5, -1.0, A.mult, A.add, ["cand"], ["thr"])
-        tt(T.sq[:], T.bst[:], T.bst[:], A.mult, ["bst"], ["sq"])
-        tt(T.dl[:], T.bst[:], x, A.subtract, ["bst", "x%d" % t], ["dl"])
-        tt(T.go[:], T.SM[:, 0:64], T.thr[:], A.is_le, ["thr"], ["SM", "go"])
-        tt(T.sq[:], T.sq[:], xx, A.subtract, ["xx%d" % t], ["sq"])
-        tt(T.gd[:, 0:64], T.go[:], T.dl[:], A.mult, ["go", "dl"], ["gd0"])
-        tt(T.gd[:, 64:128], T.go[:], T.sq[:], A.mult, ["go", "sq"], ["gd1"])
-        mms([(T.SM[:, 0:128], T.st[:, 128 * t:128 * t + 128], T.ident[:], True, False), (T.SM[:, 0:128], T.gd[:], T.ident[:], False, True)],
-            ["x%d" % t, "xx%d" % t, "gd0", "gd1"], ["SM"])
-        cp(slot(rnd, me), T.SM[:, 0:128], w=["SM", "msg"])
-        send(bcast("ax%d_%d" % (rnd, me), slot(rnd, me)), ["msg"])
+            setup_gather(1, 0, "ss")
+            setup_gather(1, 1, "ss")
+            wspread(1, 0)
+        top = T.ks[:, 15:1024:16]
+        cp(T.kq[:], top, ["ks0", "ks1"], ["kq"])
+        tt(T.cand[:, 128:192], top, T.kq[:], A.is_le, ["kq", "cand0"], ["cand"])
+        mms([(T.SM[:, 0:64], T.cand[:, 64:192], T.tri[:, 64:128], True, False), (T.SM[0:64, 0:64], T.cand[:, 128:192], T.tri[:, 0:64], False, False)]
+            + [m for d in range(1, 8) for m in ((T.SM[0:64, 0:64], T.cand[:, 128 - 8 * d:192 - 8 * d], T.ones[:, 0:64], False, False),
+                                                (T.SM[:, 0:64], T.cand[:, 64 - 8 * d:192 - 8 * d], T.ones[:, 0:64], False, d == 7))],
+            ["cand", "tri", "ones"], ["SM"])
+        tt(T.rp[:, 128:192], top, T.kq[:], A.subtract, ["kq", "rp0"], ["rp"])
+        mms([(T.PO[0:64, 0:64], T.rp[:, 128:192], T.im1[:, 0:64], False, False), (T.PO[:, 0:64], T.rp[:, 64:192], T.im1[:, 64:128], False, True)],
+            ["rp"], ["PO"])
+        ts(T.go[:], T.SM[:, 0:64], M - 199.5, None, A.is_le, w=["SM", "go"])
+        tt(T.gd[:], T.PO[:, 0:64], T.go[:], A.mult, ["go"], ["PO", "gd"])
+        msg = "msg%d" % rnd
+        tt(slot(rnd, me), T.gd[:], xold, A.add, ["gd", xkey], [msg])
+        send(bcast("ax%d_%d" % (rnd, me), slot(rnd, me)), [msg])
+
+        def later(e, q, hh):
+            update(e, q, t, hh, slot(rnd, q), [msg] if q == me else [], [] if q == me else [arr("ax%d_%d" % (rnd, q))])
         if rnd > 0:
-            ac(T.outp[0:64, t:256:2], T.SM[0:64, 0:128], F.Copy, w=["SM", "out%d" % t])
+            ac(T.outp[:, t:128:2], slot(rnd, me), F.Copy, [msg], ["out%d" % t])
         if rnd == 0:
+            setup_gather(1, 2, "vs")
             lists_pe(1, 0, "PO")
-            update("v", me, t, 0, slot(rnd, me), ["msg"], [])
-            update("v", me, t, 1, slot(rnd, me), ["msg"], [])
+        later("v", me, 0)
+        later("v", me, 1)
+        if rnd == 0:
             lists_ev(1, 0, "PO")
-            lists_pe(1, 2, "SM")
-            wprime("v", 1, 0, 0, 512)
-            wprime("v", 1, 0, 512, 512)
-            lists_ev(1, 2, "SM")
-            lists_pe(1, 1, "PO")
-            wprime("s", 1, 1, 0, 512)
-            wprime("s", 1, 1, 512, nx)
-            lists_ev(1, 1, "PO")
-            tt(T.st[:, 0:128], T.st[:, 0:128], T.gd[:], A.add, ["gd0", "gd1"], ["x0", "xx0"])
-        else:
-            update("v", me, t, 0, slot(rnd, me), ["msg"], [])
-            update("s", me, t, 1, slot(rnd, me), ["msg"], [])
-        if rnd == 1:
-            for z in range(2):
-                ac(T.zz[:, 0:1024], T.gat[:, gcol(z, 0):gcol(z, 0) + 1024], F.Identity, gkeys(z, 0) + ["wsc", "cl"],
-                   ["z0", "z512", "cl%d" % (4 + z)], scale=c[:, 5:6], accum_out=T.cl[:, 8 * me + 4 + z:8 * me + 5 + z])
         if rnd == 2:
-            dmas("y", "so", [(T.newpart[:, 256 * s:256 * s + 256], T.outp[8 * s:8 * s + 8, :]) for s in range(8)], ["out0", "out1"])
-        for q in order[1:]:
+            cv = [(0, 0, 512), (0, 512, 512), (1, 0, CV)]
+            cs = [(1, CV, 512, "K0"), (1, CV + 512, 512 - CV, "K1")]
+            for k in (2, 0, 1):
+                z, lo, n = cv[k]
+                b = bank("s")
+                mms([(T[b][:, 0:n], T.selw[:], wrow(z, 0, lo, n), True, False), (T[b][:, 0:n], ident, owncols(z, lo, n), False, True)], ownk(z), [b])
+                ac(T.zz[:, 512 * k:512 * k + n], T[b][:, 0:n], F.Relu, w=[b, "z%d" % (512 * k)], bias=-16.0)
+            for z, lo, n, b in cs:
+                mms([(T[b][:, 0:n], T.selw[:], wrow(z, 0, lo, n), True, False), (T[b][:, 0:n], ident, owncols(z, lo, n), False, False)], ownk(z), [b])
+            mms([(T.PO[0:8, 0:128], T.gw[:], wrow(s // 8, 0, 128 * (s % 8), 128), s == 0, False) for s in range(16)], ["gw"], ["PO"])
+        for n, q in enumerate(lands):
             for hh in range(2):
-                update("vs"[hh], q, t, hh, slot(rnd, q), [], [arr("ax%d_%d" % (rnd, q), q)])
+                later("vs"[hh], q, hh)
+            if rnd == 0 and n == 1:
+                lists_pe(1, 2, "SM")
+        if rnd == 0:
+            lists_ev(1, 2, "SM")
+        if rnd == 2:
+            dmas("y", "so", [(T.newpart[:, 256 * (s % 8) + 128 * (s // 8):256 * (s % 8) + 128 * (s // 8) + 128], T.outp[8 * s:8 * s + 8, :])
+                             for s in range(16)], ["out0", "out1"], (), [arr("ax2_%d" % lands[-1])])
 
-    cb = ["Y0", "Y1", "U0", "U1"]
+    def csum(src, c0, n, key, stop=False):
+        mms([(T.PO[0:8, 0:128], T.gz[:], src[:, c0 + s:c0 + s + 128], False, stop and s == n - 128) for s in range(0, n, 128)], [key, "gz"], ["PO"])
 
-    def cya(u):
-        t, lo, b = u // 2, 512 * (u % 2), cb[u]
-        mms([(T[b][:], T.selw[:], wrow(t, 0, lo, 512), True, False), (T[b][:], T.im1[:], owncols(t, lo, 512), False, False)], tabk, [b])
+    def ct(k):
+        z, lo, n = cv[k]
+        tt(T.tt[:, 512 * k:512 * k + n], look(z, 0, 0, lo, n), T.zz[:, 512 * k:512 * k + n], A.min, tabk + ["z%d" % (512 * k)], ["ct%d" % k])
 
-    def cr(u):
-        ac(T.zz[:, 512 * u:512 * u + 512], T[cb[u]][:], F.Relu, ["cl"], [cb[u], "z%d" % (512 * u), "cl%d" % u],
-           accum_out=T.cl[:, 8 * me + u:8 * me + u + 1])
+    def cu(k):
+        z, lo, n = cv[k]
+        tt(T.uu[:, 512 * k:512 * k + n], look(z, 0, 1, lo, n), T.tt[:, 512 * k:512 * k + n], A.min, tabk + ["ct%d" % k], ["cu%d" % k])
 
-    def cg(e, u, jj, stop):
-        c0 = 1024 * u + 512 * jj
-        sgather(e, u // 2, 0, jj, 512 * (u % 2), 512, c0)
-        mms([(T[cb[u]][:], T.im1[:], T.ca[:, c0:c0 + 512], False, stop)], ["ca%d" % c0], [cb[u]])
-    cya(0)
-    cg("v", 0, 0, False)
-    cg("s", 0, 1, True)
-    cya(1)
-    cg("v", 1, 0, False)
-    cg("s", 1, 1, True)
-    cya(2)
-    cya(3)
-    cg("v", 2, 0, False)
-    cg("s", 2, 1, True)
+    def cg(k, jj):
+        z, lo, n, b = cs[k]
+        sgather(z, 0, jj, lo, n, 1024 * k + 512 * jj)
+        yb(b, n, 1024 * k + 512 * jj, jj == 1)
+
+    def cr(k):
+        z, lo, n, b = cs[k]
+        ac(T.wp[:, 1024 + 512 * k:1024 + 512 * k + n], T[b][:, 0:n], F.Relu, w=[b, "cz%d" % k], bias=-48.0)
+    ct(0)
+    cg(0, 0)
+    ct(1)
+    cg(0, 1)
+    cu(0)
+    cg(1, 0)
+    csum(T.uu, 0, 512, "cu0")
+    cg(1, 1)
+    ct(2)
     cr(0)
-    cg("v", 3, 0, False)
+    cu(1)
+    csum(T.wp, 1024, 512, "cz0")
     cr(1)
-    cg("v", 3, 1, True)
-    cr(2)
-    cr(3)
-    clk = ["cl"] + ["cl%d" % u for u in range(6)]
-    send(bcast("ac", T.cl[:, 8 * me:8 * me + 8]), clk)
-    total["ac"] = sum(len(masks(q, [z for z in range(N) if z != q])[me]) for q in others)
-    mms([(T.SM[0:8, 0:8 * N], T.gz[:], T.cl[:], True, True)], ["gz"] + clk, ["SM"], [("ac", total["ac"])])
-    op("v", lambda: vec.tensor_reduce(T.cs[0:8, 0:1], T.SM[0:8, 0:8 * N], AxisListType.X, A.add), w=["SM", "cs"])
+    csum(T.uu, 512, 512, "cu1")
+    cu(2)
+    csum(T.uu, 1024, CV, "cu2")
+    csum(T.wp, 1536, 512 - CV, "cz1", True)
+    op("v", lambda: vec.tensor_reduce(T.cl[0:8, 4 * me:4 * me + 1], T.PO[0:8, 0:128], AxisListType.X, A.add), w=["PO", "cl"])
+    send(bcast("ac", T.cl[:, 4 * me:4 * me + 4]), ["cl"])
+    total["ac"] = ne * len(others)
+    wait("v", ("ac", total["ac"]))
+    op("v", lambda: vec.tensor_reduce(T.cs[0:8, 0:1], T.cl[0:8, 0:4 * N:4], AxisListType.X, A.add), ["cl"], ["cs"])
     dmas("y", "sc", [(T.cut[:], T.cs[0:8, 0:1])], ["cs"])
     for s in total:
         if s != "sc":

@@ -7,7 +7,7 @@ XV = 704
 CV = 128
 SCRATCH = {"land": ("sbuf", [128, N, 768], "bfloat16"), "sel": ("sbuf", [128, 128, 16], "bfloat16")}
 for _t, _l in (("bfloat16", dict(tab=NV, win=NV, gat=3 * V, pb=256, wp=4096, tt=2048, uu=2048, ca=4096, zz=2048, kc=512, wb=128, wt=128,
-                                 xl=R * N * 64, cand=192, rp=192, kq=64, go=64, gd=64, idw=160, kl=128, zb=144, spl=512, pq=1152,
+                                 xl=R * N * 64, cand=384, kq=64, go=64, gd=64, idw=160, kl=128, zb=144, spl=512, pq=1152,
                                  i16=128, im64=128, im1=128, tri=128, ones=192, selw=128, prm=192, zj=864, sw=512, c32=64, gz=8, gw=8, bm=128)),
                ("int32", dict(m32=384, wl=128, inc32=384, p32=256, i0=384, i1=384, row=4)),
                ("uint16", dict(ioff=384, noff=768)),
@@ -16,7 +16,7 @@ for _t, _l in (("bfloat16", dict(tab=NV, win=NV, gat=3 * V, pb=256, wp=4096, tt=
         SCRATCH[_n] = ("sbuf", [128, _l[_n]], _t)
 for _n in ("K0", "K1", "Y0", "Y1", "U0", "U1", "SM", "PO"):
     SCRATCH[_n] = ("psum", [128, 512], "float32")
-SEMAPHORES = (["cv", "cs", "cp", "cg", "ls", "ldp", "ldw", "ldi", "ldx", "wd", "so", "sc", "wz", "wr0", "wr1", "ac", "pn"]
+SEMAPHORES = (["cv", "cs", "cp", "cg", "ls", "ldp", "ldw", "ldi", "ldx", "wd", "so", "sc", "wz", "wr0", "wr1", "ac"]
               + ["pf%d" % q for q in range(N)]
               + ["ax%d_%d" % (k, q) for k in range(R) for q in range(N)] + ["pd%d_%d" % (h, q) for h in range(2) for q in range(N)])
 
@@ -161,20 +161,21 @@ def rank_program(g, core, T, topo):
     pick(T.idw[:], T.ones[:, 0:160], [[1, 160]], A.is_equal, 0.0, -16, -1, ["ones"], ["ident"])
     pick(T.prm[:], T.ones[:], [[1000, 3], [1, 8], [8, 8]], A.is_equal, 0.0, -1000, -1, ["ones"], ["prm"])
     iota(T.cj[:], [[2, 4]], 2, 0, "cj")
-    for t in range(2):
+
+    def split(t):
         for hi in range(2):
             pick(T.spl[:, 256 * t + 128 * hi:256 * t + 128 * hi + 128], T.ones[:, 0:128], [[16, 8], [1000, 2], [2, 8]], A.is_equal, 0.0,
                  t - 1000 * hi, -1, ["ones"], ["spl%d" % (2 * t + hi)])
+    split(0)
     wipe(me)
     ts(T.row[:, 1:2], T.row[:, 0:1], 16, None, A.bitwise_and, r=["row"], w=["row1"])
     ts(T.row[:, 2:3], T.row[:, 0:1], 15, None, A.bitwise_and, r=["row"], w=["row2"])
     ts(cM1, T.row[:, 1:2], 16.0, None, A.is_equal, r=["row1"], w=["m1"])
     ts(cM0, T.row[:, 1:2], 0.0, None, A.is_equal, r=["row1"], w=["m0"])
     cp(cP, T.row[:, 2:3], ["row2"], ["p"])
-    ms(T.zb[:], 0.0, "zb")
-    ms(T.cand[:, 0:128], 0.0, "cand0")
-    ms(T.rp[:, 0:128], 0.0, "rp0")
-    ms(T.cl[:, 4 * me:4 * me + 4], 0.0, "cl")
+    ac(T.sel[:, :, 0:1], ident, F.Copy, ["ident"], ["sel"])
+    ac(T.zb[:], T.ones[:, 0:144], F.Copy, ["ones"], ["zb"], scale=0.0)
+    ac(T.sel[:, :, 1:2], ident, F.Copy, ["ident"], ["sel1"])
     for gh in range(2):
         for ah in range(2):
             k, o = 2 * gh + ah, 16 - 16 * (gh - ah)
@@ -189,10 +190,12 @@ def rank_program(g, core, T, topo):
         ["pb", "prm"], ["SM"])
     ac(L[:, me, 0:128], T.SM[:, 0:128], F.Copy, w=["SM", "x"])
     cp(L[:, me, 128:256], T.dd[:, 0:128], ["d1"], ["h1"])
-    cp(T.wb[:], T.wl[:], ["wl"], ["wb"])
+    ac(T.sel[:, :, 2:4], T.sel[:, :, 0:2], F.Copy, ["sel1"], ["sel"])
+    ac(T.sel[:, :, 4:8], T.sel[:, :, 0:4], F.Copy, w=["sel"])
     tt(L[:, me, 256:384], T.dd[:, 0:128], L[:, me, 128:256], A.subtract, ["d1", "h1"], ["l1"])
-    op("v", lambda: vec.transpose(T.wt[:], T.wb[:]), ["wb"], ["wt"])
+    cp(T.wb[:], T.wl[:], ["wl"], ["wb"])
     tt(T.dd[:, 128:256], T.m32[:, 256:384], T.m32[:, 0:128], A.subtract, ["m32"], ["d2"])
+    op("v", lambda: vec.transpose(T.wt[:], T.wb[:]), ["wb"], ["wt"])
     mms([(T.PO[:, 32 * (2 * rr + ah):32 * (2 * rr + ah) + 32], T.sw[:, 128 * (2 * gh + ah):128 * (2 * gh + ah) + 128],
           T.wt[:, 64 * gh + 32 * rr:64 * gh + 32 * rr + 32], gh == 0, gh == 1) for rr in range(2) for ah in range(2) for gh in range(2)],
         ["wt"] + ["sw%d" % k for k in range(4)], ["PO"])
@@ -205,11 +208,10 @@ def rank_program(g, core, T, topo):
     def half(q, h):
         return L[:, q, 384 * h:384 * h + 384]
     for h in range(2):
-        send([([ch[h % len(ch)] for ch in far_chips(me)], far_eng, "pd%d_%d" % (h, me), half(me, h))], hkeys[h])
-    got = [{}, {}]
-    if near:
-        send([(near, near_eng, "pn", L[:, me, :])], [])
-        got[0][near[0]] = got[1][near[0]] = arr("pn")
+        s = "pd%d_%d" % (h, me)
+        send([([ch[h % len(ch)] for ch in far_chips(me)], far_eng, s, half(me, h))] + [(near, near_eng, s, half(me, h)) for q in near], hkeys[h])
+    got = [{q: arr("pd%d_%d" % (h, q)) for q in near} for h in range(2)]
+    split(1)
     pick(T.bm[:], T.ones[:, 0:128], [[-16, 8], [0, 16]], A.is_ge, 0.0, 0, 1, ["ones"], ["bm"])
     pick(T.bm[:], T.bm[:], [[16, 8], [0, 16]], A.is_ge, 0.0, 15, -1, (), ["bm"])
     iota(T.c32[:], [[32, 64]], 0, 0, "c32")
@@ -230,18 +232,14 @@ def rank_program(g, core, T, topo):
     iota(T.kc[:], [[0, 32], [-1, 16]], 16, 128, "kc")
 
     copies = come[-3:]
-    dmas("y", "wz", [(T.win[:, V * q:V * q + V], T.win[:, V * me:V * me + V]) for q in copies], ["win%d" % me, "m32", "wl"], ["win%d" % q for q in copies])
-    cp(T.sel[:, :, 0:1], ident, ["ident"], ["sel"])
+    dmas("y", "wz", [(T.win[:, V * q:V * q + V], T.win[:, V * me:V * me + V]) for q in copies], ["win%d" % me], ["win%d" % q for q in copies])
     ts(c[:, 6:9], T.cj[:, 0:3], cP, None, A.is_gt, r=["cj", "p"], w=["D1"])
-    cp(T.sel[:, :, 1:2], T.sel[:, :, 0:1], w=["sel"])
-    cp(T.sel[:, :, 2:4], T.sel[:, :, 0:2], w=["sel"])
-    tt(c[:, 9:11], c[:, 7:9], c[:, 6:8], A.subtract, ["D1"], ["D2"])
-    cp(T.sel[:, :, 4:8], T.sel[:, :, 0:4], w=["sel"])
-    tt(cD3, cD2, cD1, A.subtract, ["D1", "D2"], ["D3"])
     cp(T.sel[:, :, 8:16], T.sel[:, :, 0:8], w=["sel"])
-    for q in near + come:
-        if q not in copies:
-            wipe(q)
+    tt(c[:, 9:11], c[:, 7:9], c[:, 6:8], A.subtract, ["D1"], ["D2"])
+    ms(T.cand[:], 0.0, "cand")
+    tt(cD3, cD2, cD1, A.subtract, ["D1", "D2"], ["D3"])
+    wipe((near + come)[0])
+    ac(T.cl[:, 4 * me:4 * me + 4], T.ones[:, 0:4], F.Copy, ["ones"], ["cl"], scale=0.0)
     for out, key, k in ((T.i16, "i16", 16.0), (T.im64, "im64", -64.0), (T.im1, "im1", -1.0)):
         ac(out[:], ident, F.Copy, ["ident"], [key], scale=k)
     for t in range(2):
@@ -436,39 +434,50 @@ def rank_program(g, core, T, topo):
         if rnd == 0:
             lists_ev(0, 2, "SM", [1])
             vt(0, 0, 512)
+            sgather(t, 2, 0, 0, 512, 0)
             lists_ev(0, 0, "PO", [1])
-            vt(0, 512, 512)
+        elif rnd == 1:
+            lists_pe(1, 2, "SM", [1])
+            lists_pe(1, 0, "PO", [1])
+            vt(0, 0, 512)
+            sgather(t, 2, 0, 0, 512, 0)
+            lists_ev(1, 2, "SM", [1])
         else:
             vt(0, 0, 1024)
-        sgather(t, 2, 0, 0, 512, 0)
-        if rnd < 2:
-            lists_pe(t, 1, "SM")
-        else:
+            sgather(t, 2, 0, 0, 512, 0)
             kstart(0)
         yw("Y0", 2, 0, 512)
-        yw("Y1", 2, 512, 512)
         yb("Y0", 512, 0, False)
         sgather(t, 2, 1, 0, 512, 512)
-        yb("Y0", 512, 512, True)
-        if rnd == 1:
-            kstart(1)
         if rnd < 2:
-            lists_ev(t, 1, "SM")
-        if rnd == 0:
+            vt(0, 512, 512)
+            lists_pe(t, 1, "SM")
+        if rnd == 1:
+            lists_ev(1, 0, "PO", [1])
+        yb("Y0", 512, 512, True)
+        yw("Y1", 2, 512, 512)
+        if rnd < 2:
             vu(0, 0, 512, "t0_0")
+            lists_ev(t, 1, "SM")
             vu(0, 512, 512, "t0_512")
         vt(1, 0, XV)
-        yw("SM", 1, XV, xs)
         sgather(t, 2, 0, 512, 512, 1024)
         yb("Y1", 512, 1024, False)
+        if rnd == 1:
+            kstart(1)
+        if rnd == 2:
+            for k in range(2):
+                mms([(T["U%d" % k][:], T.selw[:], wrow(1, 0, 512 * k, 512), True, False), (T["U%d" % k][:], ident, owncols(1, 512 * k, 512), False, True)],
+                    ownk(1), ["U%d" % k])
+        yw("SM", 1, XV, xs)
         relu("Y0", T.zz[:, 0:512], 512, "z0")
-        if rnd > 0:
+        if rnd == 2:
             vu(0, 0, 512, "t0_0")
         kadd(T.zz, 0, 0, ["z0"])
         sgather(t, 2, 1, 512, 512, 1536)
         kadd(T.uu, 0, 0, ["u0_0"])
         yb("Y1", 512, 1536, True)
-        if rnd > 0:
+        if rnd == 2:
             vu(0, 512, 512, "t0_0")
         sgather(t, 1, 0, XV, xs, 2048)
         yb("SM", xs, 2048, False)
@@ -489,15 +498,18 @@ def rank_program(g, core, T, topo):
             setup_gather(1, 0, "ss")
             setup_gather(1, 1, "ss")
             wspread(1, 0)
+        if rnd == 2:
+            for k in range(2):
+                ac(T.win[:, 512 * k:512 * k + 512], T["U%d" % k][:], F.Relu, w=["U%d" % k, "win", "m%d" % k], bias=-16.0)
         top = T.ks[:, 15:1024:16]
         cp(T.kq[:], top, ["ks0", "ks1"], ["kq"])
-        tt(T.cand[:, 128:192], top, T.kq[:], A.is_le, ["kq", "cand0"], ["cand"])
+        tt(T.cand[:, 128:192], top, T.kq[:], A.is_le, ["kq"], ["cand"])
         mms([(T.SM[:, 0:64], T.cand[:, 64:192], T.tri[:, 64:128], True, False), (T.SM[0:64, 0:64], T.cand[:, 128:192], T.tri[:, 0:64], False, False)]
             + [m for d in range(1, 8) for m in ((T.SM[0:64, 0:64], T.cand[:, 128 - 8 * d:192 - 8 * d], T.ones[:, 0:64], False, False),
                                                 (T.SM[:, 0:64], T.cand[:, 64 - 8 * d:192 - 8 * d], T.ones[:, 0:64], False, d == 7))],
             ["cand", "tri", "ones"], ["SM"])
-        tt(T.rp[:, 128:192], top, T.kq[:], A.subtract, ["kq", "rp0"], ["rp"])
-        mms([(T.PO[0:64, 0:64], T.rp[:, 128:192], T.im1[:, 0:64], False, False), (T.PO[:, 0:64], T.rp[:, 64:192], T.im1[:, 64:128], False, True)],
+        tt(T.cand[:, 320:384], top, T.kq[:], A.subtract, ["kq"], ["rp"])
+        mms([(T.PO[0:64, 0:64], T.cand[:, 320:384], T.im1[:, 0:64], False, False), (T.PO[:, 0:64], T.cand[:, 256:384], T.im1[:, 64:128], False, True)],
             ["rp"], ["PO"])
         ts(T.go[:], T.SM[:, 0:64], M - 199.5, None, A.is_le, w=["SM", "go"])
         tt(T.gd[:], T.PO[:, 0:64], T.go[:], A.mult, ["go"], ["PO", "gd"])
@@ -511,39 +523,37 @@ def rank_program(g, core, T, topo):
             ac(T.outp[:, t:128:2], slot(rnd, me), F.Copy, [msg], ["out%d" % t])
         if rnd == 0:
             setup_gather(1, 2, "vs")
-            lists_pe(1, 0, "PO")
         later("v", me, 0)
+        if rnd == 0:
+            lists_pe(1, 0, "PO", [0])
         later("v", me, 1)
         if rnd == 0:
-            lists_ev(1, 0, "PO")
+            lists_ev(1, 0, "PO", [0])
+            lists_pe(1, 2, "SM", [0])
         if rnd == 2:
-            cv = [(0, 0, 512), (0, 512, 512), (1, 0, CV)]
-            cs = [(1, CV, 512, "K0"), (1, CV + 512, 512 - CV, "K1")]
-            for k in (2, 0, 1):
-                z, lo, n = cv[k]
-                b = bank("s")
-                mms([(T[b][:, 0:n], T.selw[:], wrow(z, 0, lo, n), True, False), (T[b][:, 0:n], ident, owncols(z, lo, n), False, True)], ownk(z), [b])
-                ac(T.zz[:, 512 * k:512 * k + n], T[b][:, 0:n], F.Relu, w=[b, "z%d" % (512 * k)], bias=-16.0)
-            for z, lo, n, b in cs:
-                mms([(T[b][:, 0:n], T.selw[:], wrow(z, 0, lo, n), True, False), (T[b][:, 0:n], ident, owncols(z, lo, n), False, False)], ownk(z), [b])
-            mms([(T.PO[0:8, 0:128], T.gw[:], wrow(s // 8, 0, 128 * (s % 8), 128), s == 0, False) for s in range(16)], ["gw"], ["PO"])
+            tt(T.win[:, 1024:1024 + CV], owncols(0, 0, CV), wcol(0, 0, 0, CV), A.min, ownk(0), ["m2"])
         for n, q in enumerate(lands):
             for hh in range(2):
-                later("vs"[hh], q, hh)
-            if rnd == 0 and n == 1:
-                lists_pe(1, 2, "SM")
-        if rnd == 0:
-            lists_ev(1, 2, "SM")
+                later("s" if rnd == n == 0 else "vs"[hh], q, hh)
+            if rnd == n == 0:
+                lists_ev(1, 2, "SM", [0])
         if rnd == 2:
             dmas("y", "so", [(T.newpart[:, 256 * (s % 8) + 128 * (s // 8):256 * (s % 8) + 128 * (s // 8) + 128], T.outp[8 * s:8 * s + 8, :])
                              for s in range(16)], ["out0", "out1"], (), [arr("ax2_%d" % lands[-1])])
+
+    cv = [(1, 0, 512), (1, 512, 512), (0, 0, CV)]
+    cs = [(0, CV, 512, "K0"), (0, CV + 512, 512 - CV, "K1")]
+
+    def cw(k):
+        z, lo, n, b = cs[k]
+        mms([(T[b][:, 0:n], T.selw[:], wrow(z, 0, lo, n), True, False), (T[b][:, 0:n], ident, owncols(z, lo, n), False, False)], ownk(z), [b])
 
     def csum(src, c0, n, key, stop=False):
         mms([(T.PO[0:8, 0:128], T.gz[:], src[:, c0 + s:c0 + s + 128], False, stop and s == n - 128) for s in range(0, n, 128)], [key, "gz"], ["PO"])
 
     def ct(k):
         z, lo, n = cv[k]
-        tt(T.tt[:, 512 * k:512 * k + n], look(z, 0, 0, lo, n), T.zz[:, 512 * k:512 * k + n], A.min, tabk + ["z%d" % (512 * k)], ["ct%d" % k])
+        tt(T.tt[:, 512 * k:512 * k + n], look(z, 0, 0, lo, n), T.win[:, 512 * k:512 * k + n], A.min, tabk + ["m%d" % k], ["ct%d" % k])
 
     def cu(k):
         z, lo, n = cv[k]
@@ -557,8 +567,11 @@ def rank_program(g, core, T, topo):
     def cr(k):
         z, lo, n, b = cs[k]
         ac(T.wp[:, 1024 + 512 * k:1024 + 512 * k + n], T[b][:, 0:n], F.Relu, w=[b, "cz%d" % k], bias=-48.0)
+    cw(0)
+    mms([(T.PO[0:8, 0:128], T.gw[:], wrow(s // 8, 0, 128 * (s % 8), 128), s == 0, False) for s in range(16)], ["gw"], ["PO"])
     ct(0)
     cg(0, 0)
+    cw(1)
     ct(1)
     cg(0, 1)
     cu(0)

from concourse.bass import DstId, RemoteDMATransfer
from concourse.mybir import AluOpType as A, AxisListType, ActivationFunctionType as F

N, V, M, R = 5, 2048, 96, 3
NV = N * V
XV = 704
CV = 128
SCRATCH = {"land": ("sbuf", [128, N, 768], "bfloat16"), "sel": ("sbuf", [128, 128, 16], "bfloat16")}
for _t, _l in (("bfloat16", dict(tab=NV, win=NV, gat=3 * V, pb=256, wp=4096, tt=2048, uu=2048, ca=4096, zz=2048, kc=512, wb=128, wt=128,
                                 xl=R * N * 64, cand=384, kq=64, go=64, gd=64, idw=160, kl=128, zb=144, spl=512, pq=1152,
                                 i16=128, im64=128, im1=128, tri=128, ones=192, selw=128, prm=192, zj=864, sw=512, c32=64, gz=8, gw=8, bm=128)),
               ("int32", dict(m32=384, wl=128, inc32=384, p32=256, i0=384, i1=384, row=4)),
               ("uint16", dict(ioff=384, noff=768)),
               ("float32", dict(ks=1024, rst=512, dd=256, outp=128, cl=4 * N, cs=4, col=24, cj=4))):
    for _n in _l:
        SCRATCH[_n] = ("sbuf", [128, _l[_n]], _t)
for _n in ("K0", "K1", "Y0", "Y1", "U0", "U1", "SM", "PO"):
    SCRATCH[_n] = ("psum", [128, 512], "float32")
SEMAPHORES = (["cv", "cs", "cp", "cg", "ls", "ldp", "ldw", "ldi", "ldx", "wd", "so", "sc", "wz", "wr0", "wr1", "ac"]
              + ["pf%d" % q for q in range(N)]
              + ["ax%d_%d" % (k, q) for k in range(R) for q in range(N)] + ["pd%d_%d" % (h, q) for h in range(2) for q in range(N)])


def rank_program(g, core, T, topo):
    me = T.rank_of(core)
    if me is None:
        return
    cores = list(T.cores)
    Q = {"v": g.vector, "s": g.scalar, "p": g.tensor, "g": g, "y": g.sync}
    vec, act, pe = g.vector, g.scalar, g.tensor
    total, seen, wr, rd = {}, {}, {}, {}

    def wait(q, tok):
        if seen.get((q, tok[0]), 0) < tok[1]:
            Q[q].wait_ge(T.sem[tok[0]], tok[1])
            seen[(q, tok[0])] = tok[1]

    def deps(q, r, w, toks):
        need = list(toks) + [wr[k] for k in list(r) + list(w) if k in wr]
        for k in w:
            need += rd.get(k, [])
        best = {}
        for s, n in need:
            if not (q == "p" and s == "cp"):
                best[s] = max(best.get(s, 0), n)
        for s in best:
            wait(q, (s, best[s]))

    def done(tok, r, w):
        for k in r:
            rd.setdefault(k, []).append(tok)
        for k in w:
            wr[k] = tok
            rd[k] = []

    def op(q, fn, r=(), w=(), toks=()):
        deps(q, r, w, toks)
        s = "c" + q
        fn().then_inc(T.sem[s], 1)
        total[s] = total.get(s, 0) + 1
        done((s, total[s]), r, w)

    def dmas(q, s, pairs, r=(), w=(), toks=()):
        deps(q, r, w, toks)
        for o, i in pairs:
            Q[q].dma_start(o, i).then_inc(T.sem[s], 16)
            total[s] = total.get(s, 0) + 16
        done((s, total[s]), r, w)

    def mms(lst, r, w, toks=()):
        def run():
            last = None
            for o, l, rr, a, b in lst:
                last = pe.matmul(o, l, rr, a, b)
            return last
        op("p", run, r, w, toks)

    def iota(out, pat, base, cm, key, fl=True):
        if fl:
            op("g", lambda: g.iota(out, pat, base, cm, allow_small_or_imprecise_dtypes=True), w=[key])
        else:
            op("g", lambda: g.iota(out, pat, base, cm), w=[key])

    def ts(out, in0, s1, s2, o0, o1=None, r=(), w=()):
        if o1 is None:
            op("v", lambda: vec.tensor_scalar(out, in0, s1, None, o0), r, w)
        else:
            op("v", lambda: vec.tensor_scalar(out, in0, s1, s2, o0, o1), r, w)

    def tt(out, in0, in1, o, r=(), w=()):
        op("v", lambda: vec.tensor_tensor(out, in0, in1, o), r, w)

    def cp(out, in_, r=(), w=()):
        op("v", lambda: vec.tensor_copy(out, in_), r, w)

    def ms(out, c, key):
        op("v", lambda: vec.memset(out, c), w=[key])

    def ac(out, in_, f, r=(), w=(), **kw):
        op("s", lambda: act.activation(out, in_, f, **kw), r, w)

    chips = sorted(set(topo.chip(x) for x in cores))

    def chip_ranks(q):
        return [x for x in range(N) if topo.chip(cores[x]) == topo.chip(cores[q])]

    def far_chips(q):
        k = chips.index(topo.chip(cores[q]))
        return [[x for x in range(N) if topo.chip(cores[x]) == ch] for ch in chips[k + 1:] + chips[:k]]

    def far_order(q):
        k = chip_ranks(q).index(q)
        fc = [c[k % len(c):] + c[:k % len(c)] for c in far_chips(q)]
        return [c[n] for n in range(2) for c in fc if n < len(c)]

    others = [q for q in range(N) if q != me]
    mine = chip_ranks(me)
    near = [q for q in mine if q != me]
    far = far_order(me)
    far_eng = topo.engines(core, cores[far[0]])
    near_eng = [e for q in near for e in topo.engines(core, cores[q]) if e not in far_eng]
    ne = len(far_eng)

    def send(items, r, toks=()):
        deps("g", r, (), toks)
        tr = []
        for ds, eng, s, ap in items:
            ids = []
            for d in ds:
                assert topo.may_write(core, cores[d])
                rid, pid, _ = topo.addr(cores[d])
                ids.append(DstId(rid=rid, pnc=pid))
            tr.append(RemoteDMATransfer(dst_ids=ids, dma_engine_mask=sum(1 << e for e in eng), remote_sem=T.sem[s], srcs=[ap], dsts=[ap] * len(ds)))
            total["ls"] = total.get("ls", 0) + len(eng)
        g.remote_dma_fused(tr, local_sem=T.sem.ls)

    def bcast(sem, ap):
        return [(far, far_eng, sem, ap)] + ([(near, near_eng, sem, ap)] if near else [])

    def arr(sem):
        total[sem] = ne
        return (sem, ne)

    dmas("y", "ldx", [(T.p32[0:64, :], T.part[:])], w=["p32"])
    dmas("s", "ldp", [(T.m32[:], T.pin[:])], w=["m32"])
    dmas("y", "ldw", [(T.wl[:, 64 * u:64 * u + 64], T.w[u:8:2, :]) for u in range(2)], w=["wl"])
    dmas("y", "ldi", [(T.inc32[:], T.inc[:])], w=["inc32"])
    c = T.col
    cP, cB, cM0, cM1, cK0, cK1, cD1, cL1, cL2, cD2, cW, cD3 = [c[:, k:k + 1] for k in range(12)]
    cU2 = [c[:, 16:17], c[:, 17:18]]
    ident = T.idw[:, 16:144]

    def pick(out, in_, pat, cmp, fill, base, cm, r, w):
        op("g", lambda: g.affine_select(out, in_, pat, cmp, fill, base, cm), r, w)

    def wipe(q):
        ms(T.win[:, V * q:V * q + V], 0.0, "win%d" % q)

    ms(T.ones[:], 1.0, "ones")
    iota(T.row[:, 0:1], [[0, 1]], 0, 1, "row", False)
    pick(T.idw[:], T.ones[:, 0:160], [[1, 160]], A.is_equal, 0.0, -16, -1, ["ones"], ["ident"])
    pick(T.prm[:], T.ones[:], [[1000, 3], [1, 8], [8, 8]], A.is_equal, 0.0, -1000, -1, ["ones"], ["prm"])
    iota(T.cj[:], [[2, 4]], 2, 0, "cj")

    def split(t):
        for hi in range(2):
            pick(T.spl[:, 256 * t + 128 * hi:256 * t + 128 * hi + 128], T.ones[:, 0:128], [[16, 8], [1000, 2], [2, 8]], A.is_equal, 0.0,
                 t - 1000 * hi, -1, ["ones"], ["spl%d" % (2 * t + hi)])
    split(0)
    wipe(me)
    ts(T.row[:, 1:2], T.row[:, 0:1], 16, None, A.bitwise_and, r=["row"], w=["row1"])
    ts(T.row[:, 2:3], T.row[:, 0:1], 15, None, A.bitwise_and, r=["row"], w=["row2"])
    ts(cM1, T.row[:, 1:2], 16.0, None, A.is_equal, r=["row1"], w=["m1"])
    ts(cM0, T.row[:, 1:2], 0.0, None, A.is_equal, r=["row1"], w=["m0"])
    cp(cP, T.row[:, 2:3], ["row2"], ["p"])
    ac(T.sel[:, :, 0:1], ident, F.Copy, ["ident"], ["sel"])
    ac(T.zb[:], T.ones[:, 0:144], F.Copy, ["ones"], ["zb"], scale=0.0)
    ac(T.sel[:, :, 1:2], ident, F.Copy, ["ident"], ["sel1"])
    for gh in range(2):
        for ah in range(2):
            k, o = 2 * gh + ah, 16 - 16 * (gh - ah)
            ac(T.sw[:, 128 * k:128 * k + 128], T.idw[:, o:o + 128], F.Identity, ["ident", "m0", "m1"], ["sw%d" % k], scale=[cM0, cM1][ah])
    ac(cB, cP, F.Identity, ["p"], ["bias"], scale=-16.0)

    L = T.land
    cp(T.pb[0:64, :], T.p32[0:64, :], ["p32"], ["pb"])
    tt(T.dd[:, 0:128], T.m32[:, 128:256], T.m32[:, 0:128], A.subtract, ["m32"], ["d1"])
    mms([m for t in range(2) for m in ((T.SM[:, 64 * t:64 * t + 64], T.prm[0:64, 0:128], T.pb[0:64, 128 + t:256:2], True, False),
                                       (T.SM[:, 64 * t:64 * t + 64], T.prm[0:64, 64:192], T.pb[0:64, t:128:2], False, True))],
        ["pb", "prm"], ["SM"])
    ac(L[:, me, 0:128], T.SM[:, 0:128], F.Copy, w=["SM", "x"])
    cp(L[:, me, 128:256], T.dd[:, 0:128], ["d1"], ["h1"])
    ac(T.sel[:, :, 2:4], T.sel[:, :, 0:2], F.Copy, ["sel1"], ["sel"])
    ac(T.sel[:, :, 4:8], T.sel[:, :, 0:4], F.Copy, w=["sel"])
    tt(L[:, me, 256:384], T.dd[:, 0:128], L[:, me, 128:256], A.subtract, ["d1", "h1"], ["l1"])
    cp(T.wb[:], T.wl[:], ["wl"], ["wb"])
    tt(T.dd[:, 128:256], T.m32[:, 256:384], T.m32[:, 0:128], A.subtract, ["m32"], ["d2"])
    op("v", lambda: vec.transpose(T.wt[:], T.wb[:]), ["wb"], ["wt"])
    mms([(T.PO[:, 32 * (2 * rr + ah):32 * (2 * rr + ah) + 32], T.sw[:, 128 * (2 * gh + ah):128 * (2 * gh + ah) + 128],
          T.wt[:, 64 * gh + 32 * rr:64 * gh + 32 * rr + 32], gh == 0, gh == 1) for rr in range(2) for ah in range(2) for gh in range(2)],
        ["wt"] + ["sw%d" % k for k in range(4)], ["PO"])
    cp(L[:, me, 384:512], T.dd[:, 128:256], ["d2"], ["h2"])
    for k in range(4):
        ac(L[:, me, 640 + k:768:4], T.PO[:, 32 * k:32 * k + 32], F.Copy, ["PO"], ["ww%d" % k])
    tt(L[:, me, 512:640], T.dd[:, 128:256], L[:, me, 384:512], A.subtract, ["d2", "h2"], ["l2"])
    hkeys = [["x", "h1", "l1"], ["h2", "l2"] + ["ww%d" % k for k in range(4)]]

    def half(q, h):
        return L[:, q, 384 * h:384 * h + 384]
    for h in range(2):
        s = "pd%d_%d" % (h, me)
        send([([ch[h % len(ch)] for ch in far_chips(me)], far_eng, s, half(me, h))] + [(near, near_eng, s, half(me, h)) for q in near], hkeys[h])
    got = [{q: arr("pd%d_%d" % (h, q)) for q in near} for h in range(2)]
    split(1)
    pick(T.bm[:], T.ones[:, 0:128], [[-16, 8], [0, 16]], A.is_ge, 0.0, 0, 1, ["ones"], ["bm"])
    pick(T.bm[:], T.bm[:], [[16, 8], [0, 16]], A.is_ge, 0.0, 15, -1, (), ["bm"])
    iota(T.c32[:], [[32, 64]], 0, 0, "c32")
    come = sorted(far, key=lambda q: [topo.chip(cores[ch[0]]) for ch in far_chips(q)].index(topo.chip(core)))
    hs = [0, 1]
    if near:
        h = mine.index(me)
        hs = [h, 1 - h]
        for q in come:
            got[h][q] = arr("pd%d_%d" % (h, q))
            send([(near, near_eng, "pf%d" % q, half(q, h))], [], [got[h][q]])
            got[1 - h][q] = arr("pf%d" % q)
    else:
        for q in come:
            for h in range(2):
                got[h][q] = arr("pd%d_%d" % (h, q))
    iota(T.rst[:], [[0, 32], [20000, 16]], 0, 0, "rst")
    iota(T.kc[:], [[0, 32], [-1, 16]], 16, 128, "kc")

    copies = come[-3:]
    dmas("y", "wz", [(T.win[:, V * q:V * q + V], T.win[:, V * me:V * me + V]) for q in copies], ["win%d" % me], ["win%d" % q for q in copies])
    ts(c[:, 6:9], T.cj[:, 0:3], cP, None, A.is_gt, r=["cj", "p"], w=["D1"])
    cp(T.sel[:, :, 8:16], T.sel[:, :, 0:8], w=["sel"])
    tt(c[:, 9:11], c[:, 7:9], c[:, 6:8], A.subtract, ["D1"], ["D2"])
    ms(T.cand[:], 0.0, "cand")
    tt(cD3, cD2, cD1, A.subtract, ["D1", "D2"], ["D3"])
    wipe((near + come)[0])
    ac(T.cl[:, 4 * me:4 * me + 4], T.ones[:, 0:4], F.Copy, ["ones"], ["cl"], scale=0.0)
    for out, key, k in ((T.i16, "i16", 16.0), (T.im64, "im64", -64.0), (T.im1, "im1", -1.0)):
        ac(out[:], ident, F.Copy, ["ident"], [key], scale=k)
    for t in range(2):
        ac(cU2[t], cP, F.Identity, ["p"], ["u%d" % t], scale=2.0, bias=float(V * me + t))
    ac(cK1, T.idw[:, 17:18], F.Identity, ["ident"], ["k1"], scale=96.0)
    ac(cK0, T.idw[:, 16:17], F.Identity, ["ident", "k1"], ["k0"], scale=-95.0, bias=cK1)
    ac(T.kl[:], T.ones[:, 0:128], F.Identity, ["ones", "k0"], ["kl"], scale=cK0)
    pick(T.tri[:], T.ones[:, 0:128], [[1, 128]], A.is_ge, 0.0, 0, -1, ["ones"], ["tri"])
    pick(T.tri[:], T.tri[:], [[1, 128]], A.not_equal, -199.0, 0, -1, (), ["tri"])

    def by_group():
        ac(T.zb[:, 15:143:16], T.bm[:, 0:128:16], F.Copy, ["bm"], ["zb"])
        ac(T.selw[:], T.bm[:], F.Identity, ["bm", "D2"], ["selw"], scale=cW)
        for k, col in enumerate((cD1, cD2, cD3)):
            ac(T.zj[:, 144 * k:144 * k + 144], T.zb[:], F.Identity, ["zb", "D1", "D2", "D3"], ["zj%d" % k], scale=col)
        ac(T.gz[:], T.bm[:, 0:128:16], F.Copy, ["bm"], ["gz"], scale=-1.0)
        ac(T.gw[:], T.selw[:, 0:128:16], F.Copy, ["selw"], ["gw"], scale=15.0)
        ts(T.zj[:, 432:864], T.zj[:, 0:432], -1.0, None, A.mult, r=["zj0", "zj1", "zj2"], w=["zjm"])

    units = [(q, h) for q in [me] + near for h in range(2)] + [(q, h) for h in hs for q in come]
    for q, h in units:
        deps("y", hkeys[h], ["win%d" % q], [] if q == me else [got[h][q]])
        for f in ((0, 1), (2, 3, 4))[h]:
            g.sync.dma_start(T.win[f:128:16, V * q:V * q + V], L[:, q, 128 * f + 128:128 * f + 256]).then_inc(T.sem.wd, 16)
            total["wd"] = total.get("wd", 0) + 16
    done(("wd", total["wd"]), (), ["win"])

    tabk = ["tab%d_%d_%d" % (q, t, hh) for q in range(N) for t in range(2) for hh in range(2)]
    flip = {"v": 0, "s": 0}

    def bank(e):
        flip[e] ^= 1
        return ("U%d" if e == "v" else "Y%d") % flip[e]

    def update(e, q, t, hh, src, keys, toks):
        b = bank(e)
        mms([(T[b][:, 128 * s + 64 * nh:128 * s + 64 * nh + 64], T.sel[:, 8 * (8 * nh + 4 * hh + s):8 * (8 * nh + 4 * hh + s) + 8, :],
              src, True, True) for s in range(4) for nh in range(2)], ["sel"] + keys, [b], toks)
        out = T.tab[:, V * q + 1024 * hh + t:V * q + 1024 * hh + 1024:2]
        key = "tab%d_%d_%d" % (q, t, hh)
        if e == "v":
            ts(out, T[b][:], cP, 16.0, A.not_equal, A.mult, ["p"], [b, key])
        else:
            ac(out, T[b][:], F.Abs, ["bias"], [b, key], bias=cB, scale=16.0)

    def first(e, q, t, hh):
        update(e, q, t, hh, L[:, q, 64 * t:64 * t + 64], ["x"] if q == me else [], [] if q == me else [got[0][q]])

    rest = [(q, k // 2, k % 2) for q in near + come for k in range(4)]
    ts(T.i0[:], T.inc32[:], 15, None, A.bitwise_and, r=["inc32"], w=["i0"])
    ts(T.i1[:], T.inc32[:], 2032, None, A.bitwise_and, r=["inc32"], w=["i1"])
    ts(T.pq[:, 0:384], T.inc32[:], 393216.0 - 1023.5, None, A.add, r=["inc32"], w=["pq0"])
    ts(T.pq[:, 384:768], T.i0[:], 128.0, None, A.mult, r=["i0"], w=["pq1"])
    ts(T.pq[:, 768:1152], T.i1[:], 0.0625, None, A.mult, r=["i1"], w=["pq2"])
    first("v", me, 0, 0)
    first("v", me, 0, 1)
    for u in rest[:2]:
        first("s", *u)
    mms([(T.PO[:, 192 * z:192 * z + 192], T.spl[:, 256 * z + 128 * hi:256 * z + 128 * hi + 128], T.pq[:, 384 * k + hi:384 * k + 384:2],
          hi + k == 0, hi + k == 3) for z in range(2) for k in range(3) for hi in range(2)],
        ["pq0", "pq1", "pq2"] + ["spl%d" % z for z in range(4)], ["PO"])
    by_group()
    for k in range(2):
        first("s", *rest[2 + k])
        first("v", me, 1, k)
    ts(T.ioff[:], T.PO[:, 0:384], -393216.0, None, A.add, w=["PO", "ioff"])
    for n, u in enumerate(rest[4:]):
        first("sv"[n % 2], *u)

    def ncol(t, i, jj):
        return 384 * t + 128 * i + 64 * jj

    def gkeys(t, i):
        return ["g%d_%d_0" % (t, i), "g%d_%d_1" % (t, i)]

    def gcol(t, i):
        return 3072 * t + 1024 * i

    def setup_gather(t, i, e):
        w, g0, o = T.win[:, 0:NV], gcol(t, i), 192 * t + 64 * i
        for z in range(2):
            out, src = T.gat[:, g0 + 512 * z:g0 + 512 * z + 512], w.indirect(T.ioff[:, o + 32 * z:o + 32 * z + 32])
            if e[z] == "v":
                cp(out, src, ["win", "ioff"], gkeys(t, i)[z:z + 1])
            else:
                ac(out, src, F.Copy, ["win", "ioff"], gkeys(t, i)[z:z + 1])

    DIFF = ((0, 1), (3, 2), (4, 5))

    def lists_pe(t, i, b, js=(0, 1)):
        lst = []
        for jj in js:
            out, j = T[b][:, 64 * jj:64 * jj + 64], DIFF[i][jj]
            lst.append((out, ident, T.c32[:], True, False))
            lst += [(out, T.zj[:, 144 * j + 15 - a:144 * j + 143 - a], T.gat[:, gcol(t, i) + a:gcol(t, i) + 1024:16], False, a == 15) for a in range(16)]
        mms(lst, gkeys(t, i) + ["zj0", "zj1", "zj2", "zjm", "c32", "ident"], [b])

    def lists_ev(t, i, b, js=(0, 1)):
        ts(T.noff[:, ncol(t, i, js[0]):ncol(t, i, js[-1]) + 64], T[b][:, 64 * js[0]:64 * js[-1] + 64], cU2[t], None, A.add,
           r=["u%d" % t], w=[b] + ["n%d_%d_%d" % (t, i, jj) for jj in js])

    def wrow(t, i, lo, n):
        return T.gat[:, gcol(t, i) + lo:gcol(t, i) + lo + n]

    def wcol(t, i, lo, n):
        return T.wp[:, 2048 * t + 1024 * i + lo:2048 * t + 1024 * i + lo + n]

    def wkeys(t, i):
        return ["w%d_%d_0" % (t, i), "w%d_%d_512" % (t, i)]

    def wprime(e, t, i, lo, n):
        b = bank(e)
        mms([(T[b][:, 0:n], T.selw[:], wrow(t, i, lo, n), True, True)], gkeys(t, i) + ["selw"], [b])
        key = "w%d_%d_%d" % (t, i, lo)
        if e == "v":
            cp(wcol(t, i, lo, n), T[b][:, 0:n], w=[b, key])
        else:
            ac(wcol(t, i, lo, n), T[b][:, 0:n], F.Copy, w=[b, key])

    def wspread(t, i0):
        n = 1024 * (1 - i0) + XV
        dmas("y", "wr%d" % t, [(T.wp[p:128:16, 2048 * t + 1024 * i0:2048 * t + 1024 * i0 + n], T.gat[4:128:16, gcol(t, i0):gcol(t, i0) + n]) for p in range(16)],
             [k for i in range(i0, 2) for k in gkeys(t, i)], [k for i in range(i0, 2) for k in wkeys(t, i)])

    def slot(k, q):
        return T.xl[:, (k * N + q) * 64:(k * N + q + 1) * 64]

    def look(t, i, jj, lo, n):
        return T.tab[:, 0:NV].indirect(T.noff[:, ncol(t, i, jj) + lo // 16:ncol(t, i, jj) + (lo + n) // 16])

    def owncols(t, lo, n):
        return T.tab[:, V * me + 2 * lo + t:V * me + 2 * (lo + n):2]

    def ownk(t):
        return [k for k in tabk if k.startswith("tab%d_%d" % (me, t))]

    def sgather(t, i, jj, lo, n, c0):
        ac(T.ca[:, c0:c0 + n], look(t, i, jj, lo, n), F.Sign, tabk + ["n%d_%d_%d" % (t, i, jj)], ["ca%d" % c0])

    def yb(b, n, c0, stop):
        mms([(T[b][:, 0:n], T.i16[:], T.ca[:, c0:c0 + n], False, stop)], ["ca%d" % c0, "i16"], [b])

    def kstart(t):
        for h in range(2):
            b = "K%d" % h
            mms([(T[b][:], T.kl[:], T.kc[:], True, False)]
                + [(T[b][:, 128 * s:128 * s + 128], owncols(t, 512 * h + 128 * s, 128), T.im1[:], False, False) for s in range(4)],
                ["kl", "kc", "im1"] + ownk(t), [b])

    kstart(0)
    setup_gather(0, 0, "vs")
    setup_gather(0, 2, "vs")
    lists_pe(0, 0, "SM", [0])
    setup_gather(0, 1, "vs")
    wspread(0, 1)
    lists_ev(0, 0, "SM", [0])
    wprime("s", 0, 0, 0, 512)
    lists_pe(0, 2, "PO", [0])
    lists_ev(0, 2, "PO", [0])
    wprime("v", 0, 0, 512, 512)
    lists_pe(0, 2, "SM", [1])
    lists_pe(0, 0, "PO", [1])

    lands = near + sorted(far, key=lambda q: far_order(q).index(me))
    xs = 1024 - XV
    for rnd in range(R):
        t = rnd % 2
        xold, xkey = (L[:, me, 64 * t:64 * t + 64], "x") if rnd < 2 else (slot(0, me), "msg0")

        def vt(i, lo, n):
            tt(T.tt[:, 1024 * i + lo:1024 * i + lo + n], look(t, i, 0, lo, n), wcol(t, i, lo, n),
               A.min, tabk + ["n%d_%d_0" % (t, i)] + wkeys(t, i), ["t%d_%d" % (i, lo)])

        def vu(i, lo, n, tk):
            tt(T.uu[:, 1024 * i + lo:1024 * i + lo + n], look(t, i, 1, lo, n), T.tt[:, 1024 * i + lo:1024 * i + lo + n],
               A.min, tabk + ["n%d_%d_1" % (t, i), tk], ["u%d_%d" % (i, lo)])

        def kadd(src, c0, lo, keys, stop=False):
            b = "K%d" % (lo // 512)
            mms([(T[b][:, s:s + 128], src[:, c0 + s:c0 + s + 128], T.im64[:], False, stop and s == 384) for s in range(0, 512, 128)], keys + ["im64"], [b])

        def yw(b, i, lo, n):
            mms([(T[b][:, 0:n], T.selw[:], wrow(t, i, lo, n), True, False)], gkeys(t, i) + ["selw"], [b])

        def relu(b, out, n, key):
            ac(out, T[b][:, 0:n], F.Relu, w=[b, key], bias=-32.0)

        def scan(h):
            b = "K%d" % h
            op("v", lambda: vec.tensor_tensor_scan(T.ks[:, 512 * h:512 * h + 512], T.rst[:], T[b][:], 0.0, A.min, A.max), ["rst"], [b, "ks%d" % h])

        if rnd == 0:
            lists_ev(0, 2, "SM", [1])
            vt(0, 0, 512)
            sgather(t, 2, 0, 0, 512, 0)
            lists_ev(0, 0, "PO", [1])
        elif rnd == 1:
            lists_pe(1, 2, "SM", [1])
            lists_pe(1, 0, "PO", [1])
            vt(0, 0, 512)
            sgather(t, 2, 0, 0, 512, 0)
            lists_ev(1, 2, "SM", [1])
        else:
            vt(0, 0, 1024)
            sgather(t, 2, 0, 0, 512, 0)
            kstart(0)
        yw("Y0", 2, 0, 512)
        yb("Y0", 512, 0, False)
        sgather(t, 2, 1, 0, 512, 512)
        if rnd < 2:
            vt(0, 512, 512)
            lists_pe(t, 1, "SM")
        if rnd == 1:
            lists_ev(1, 0, "PO", [1])
        yb("Y0", 512, 512, True)
        yw("Y1", 2, 512, 512)
        if rnd < 2:
            vu(0, 0, 512, "t0_0")
            lists_ev(t, 1, "SM")
            vu(0, 512, 512, "t0_512")
        vt(1, 0, XV)
        sgather(t, 2, 0, 512, 512, 1024)
        yb("Y1", 512, 1024, False)
        if rnd == 1:
            kstart(1)
        if rnd == 2:
            for k in range(2):
                mms([(T["U%d" % k][:], T.selw[:], wrow(1, 0, 512 * k, 512), True, False), (T["U%d" % k][:], ident, owncols(1, 512 * k, 512), False, True)],
                    ownk(1), ["U%d" % k])
        yw("SM", 1, XV, xs)
        relu("Y0", T.zz[:, 0:512], 512, "z0")
        if rnd == 2:
            vu(0, 0, 512, "t0_0")
        kadd(T.zz, 0, 0, ["z0"])
        sgather(t, 2, 1, 512, 512, 1536)
        kadd(T.uu, 0, 0, ["u0_0"])
        yb("Y1", 512, 1536, True)
        if rnd == 2:
            vu(0, 512, 512, "t0_0")
        sgather(t, 1, 0, XV, xs, 2048)
        yb("SM", xs, 2048, False)
        sgather(t, 1, 1, XV, xs, 2560)
        kadd(T.uu, 512, 512, ["u0_512"])
        yb("SM", xs, 2560, True)
        vu(1, 0, 512, "t1_0")
        relu("Y1", T.zz[:, 512:1024], 512, "z512")
        kadd(T.uu, 1024, 0, ["u1_0"], True)
        vu(1, 512, XV - 512, "t1_0")
        kadd(T.zz, 512, 512, ["z512"])
        relu("SM", T.uu[:, 1024 + XV:2048], xs, "u1_x")
        scan(0)
        kadd(T.uu, 1536, 512, ["u1_512", "u1_x"], True)
        mms([(T.PO[:, 0:64], T.im1[:], xold, True, False)], [xkey, "im1"], ["PO"])
        scan(1)
        if rnd == 0:
            setup_gather(1, 0, "ss")
            setup_gather(1, 1, "ss")
            wspread(1, 0)
        if rnd == 2:
            for k in range(2):
                ac(T.win[:, 512 * k:512 * k + 512], T["U%d" % k][:], F.Relu, w=["U%d" % k, "win", "m%d" % k], bias=-16.0)
        top = T.ks[:, 15:1024:16]
        cp(T.kq[:], top, ["ks0", "ks1"], ["kq"])
        tt(T.cand[:, 128:192], top, T.kq[:], A.is_le, ["kq"], ["cand"])
        mms([(T.SM[:, 0:64], T.cand[:, 64:192], T.tri[:, 64:128], True, False), (T.SM[0:64, 0:64], T.cand[:, 128:192], T.tri[:, 0:64], False, False)]
            + [m for d in range(1, 8) for m in ((T.SM[0:64, 0:64], T.cand[:, 128 - 8 * d:192 - 8 * d], T.ones[:, 0:64], False, False),
                                                (T.SM[:, 0:64], T.cand[:, 64 - 8 * d:192 - 8 * d], T.ones[:, 0:64], False, d == 7))],
            ["cand", "tri", "ones"], ["SM"])
        tt(T.cand[:, 320:384], top, T.kq[:], A.subtract, ["kq"], ["rp"])
        mms([(T.PO[0:64, 0:64], T.cand[:, 320:384], T.im1[:, 0:64], False, False), (T.PO[:, 0:64], T.cand[:, 256:384], T.im1[:, 64:128], False, True)],
            ["rp"], ["PO"])
        ts(T.go[:], T.SM[:, 0:64], M - 199.5, None, A.is_le, w=["SM", "go"])
        tt(T.gd[:], T.PO[:, 0:64], T.go[:], A.mult, ["go"], ["PO", "gd"])
        msg = "msg%d" % rnd
        tt(slot(rnd, me), T.gd[:], xold, A.add, ["gd", xkey], [msg])
        send(bcast("ax%d_%d" % (rnd, me), slot(rnd, me)), [msg])

        def later(e, q, hh):
            update(e, q, t, hh, slot(rnd, q), [msg] if q == me else [], [] if q == me else [arr("ax%d_%d" % (rnd, q))])
        if rnd > 0:
            ac(T.outp[:, t:128:2], slot(rnd, me), F.Copy, [msg], ["out%d" % t])
        if rnd == 0:
            setup_gather(1, 2, "vs")
        later("v", me, 0)
        if rnd == 0:
            lists_pe(1, 0, "PO", [0])
        later("v", me, 1)
        if rnd == 0:
            lists_ev(1, 0, "PO", [0])
            lists_pe(1, 2, "SM", [0])
        if rnd == 2:
            tt(T.win[:, 1024:1024 + CV], owncols(0, 0, CV), wcol(0, 0, 0, CV), A.min, ownk(0), ["m2"])
        for n, q in enumerate(lands):
            for hh in range(2):
                later("s" if rnd == n == 0 else "vs"[hh], q, hh)
            if rnd == n == 0:
                lists_ev(1, 2, "SM", [0])
        if rnd == 2:
            dmas("y", "so", [(T.newpart[:, 256 * (s % 8) + 128 * (s // 8):256 * (s % 8) + 128 * (s // 8) + 128], T.outp[8 * s:8 * s + 8, :])
                             for s in range(16)], ["out0", "out1"], (), [arr("ax2_%d" % lands[-1])])

    cv = [(1, 0, 512), (1, 512, 512), (0, 0, CV)]
    cs = [(0, CV, 512, "K0"), (0, CV + 512, 512 - CV, "K1")]

    def cw(k):
        z, lo, n, b = cs[k]
        mms([(T[b][:, 0:n], T.selw[:], wrow(z, 0, lo, n), True, False), (T[b][:, 0:n], ident, owncols(z, lo, n), False, False)], ownk(z), [b])

    def csum(src, c0, n, key, stop=False):
        mms([(T.PO[0:8, 0:128], T.gz[:], src[:, c0 + s:c0 + s + 128], False, stop and s == n - 128) for s in range(0, n, 128)], [key, "gz"], ["PO"])

    def ct(k):
        z, lo, n = cv[k]
        tt(T.tt[:, 512 * k:512 * k + n], look(z, 0, 0, lo, n), T.win[:, 512 * k:512 * k + n], A.min, tabk + ["m%d" % k], ["ct%d" % k])

    def cu(k):
        z, lo, n = cv[k]
        tt(T.uu[:, 512 * k:512 * k + n], look(z, 0, 1, lo, n), T.tt[:, 512 * k:512 * k + n], A.min, tabk + ["ct%d" % k], ["cu%d" % k])

    def cg(k, jj):
        z, lo, n, b = cs[k]
        sgather(z, 0, jj, lo, n, 1024 * k + 512 * jj)
        yb(b, n, 1024 * k + 512 * jj, jj == 1)

    def cr(k):
        z, lo, n, b = cs[k]
        ac(T.wp[:, 1024 + 512 * k:1024 + 512 * k + n], T[b][:, 0:n], F.Relu, w=[b, "cz%d" % k], bias=-48.0)
    cw(0)
    mms([(T.PO[0:8, 0:128], T.gw[:], wrow(s // 8, 0, 128 * (s % 8), 128), s == 0, False) for s in range(16)], ["gw"], ["PO"])
    ct(0)
    cg(0, 0)
    cw(1)
    ct(1)
    cg(0, 1)
    cu(0)
    cg(1, 0)
    csum(T.uu, 0, 512, "cu0")
    cg(1, 1)
    ct(2)
    cr(0)
    cu(1)
    csum(T.wp, 1024, 512, "cz0")
    cr(1)
    csum(T.uu, 512, 512, "cu1")
    cu(2)
    csum(T.uu, 1024, CV, "cu2")
    csum(T.wp, 1536, 512 - CV, "cz1", True)
    op("v", lambda: vec.tensor_reduce(T.cl[0:8, 4 * me:4 * me + 1], T.PO[0:8, 0:128], AxisListType.X, A.add), w=["PO", "cl"])
    send(bcast("ac", T.cl[:, 4 * me:4 * me + 4]), ["cl"])
    total["ac"] = ne * len(others)
    wait("v", ("ac", total["ac"]))
    op("v", lambda: vec.tensor_reduce(T.cs[0:8, 0:1], T.cl[0:8, 0:4 * N:4], AxisListType.X, A.add), ["cl"], ["cs"])
    dmas("y", "sc", [(T.cut[:], T.cs[0:8, 0:1])], ["cs"])
    for s in total:
        if s != "sc":
            wait("g", (s, total[s]))
    wait("g", ("sc", total["sc"]))
